import numpy as np
import ml_dtypes


def mxq(x, axis, fmt="e4m3"):
    dtype, down = {"e4m3": (ml_dtypes.float8_e4m3fn, 7), "e5m2": (ml_dtypes.float8_e5m2, 14)}[fmt]
    v = np.moveaxis(np.asarray(x, np.float32).astype(ml_dtypes.bfloat16).astype(np.float64), axis, -1)
    blocks = v.reshape(v.shape[:-1] + (-1, 32))
    amax = np.abs(blocks).max(-1, keepdims=True)
    byte = np.maximum(np.where(amax > 0, np.frexp(amax)[1] - 1 + 127, 0) - down, 1)
    scale = np.exp2(byte - 127.0)
    codes = (blocks / scale).astype(np.float32).astype(dtype).astype(np.float64)
    return np.moveaxis((codes * scale).reshape(v.shape), -1, axis)


WIDE = False


def mx_kscale(k):
    if not WIDE:
        return np.ones(k)
    levels = np.array([10, -10, 5, -5, 0])
    if k % 512:
        return np.exp2(np.random.permutation(np.resize(levels, k // 32))).repeat(32)
    a = np.empty((k // 512, 16))
    for p in range(k // 512):
        a[p, :8] = np.random.permutation(np.resize(levels, 8))
        for g in range(8):
            far = levels[np.abs(levels - a[p, g]) >= 10]
            a[p, g + 8] = far[np.random.randint(len(far))]
    return np.exp2(a.ravel()).repeat(32)


def f64(x):
    return np.asarray(x).astype(np.float64)


def striped(idx):
    return np.tile(idx.reshape(-1, 16).T, (8, 1)).astype(np.uint16)


def unstriped(offs):
    return offs[:16].T.reshape(-1).astype(np.int64)


E2M1 = np.array([0.0, 0.5, 1.0, 1.5, 2.0, 3.0, 4.0, 6.0, -0.0, -0.5, -1.0, -1.5, -2.0, -3.0, -4.0, -6.0])


def pack_weight(w, fmt):
    k, n = w.shape
    w = f64(np.asarray(w, np.float32).astype(ml_dtypes.bfloat16)).reshape(k // 32, 32, n)
    amax = np.abs(w).max(1)
    if fmt == "e4m3":
        byte = np.frexp(amax)[1] - 1 + 127 - 7
    else:
        mant, ex = np.frexp(amax / 6.0)
        byte = np.where(mant > 0.5, ex, ex - 1) + 127
    byte = np.clip(np.where(amax > 0, byte, 1), 1, 254)
    scaled = (w * np.exp2(127.0 - byte)[:, None, :]).reshape(k, n).astype(np.float32)
    by_word = np.ascontiguousarray(scaled.reshape(k // 512, 128, 4, n).transpose(0, 1, 3, 2))
    if fmt == "e4m3":
        words = by_word.astype(ml_dtypes.float8_e4m3fn).view(np.uint8)
    else:
        c = by_word.astype(ml_dtypes.float4_e2m1fn).view(np.uint8) & 0xF
        words = (c[..., 0::2] | (c[..., 1::2] << 4)).reshape(k // 512, 128, 2 * n)
    return np.ascontiguousarray(words), np.ascontiguousarray(byte.astype(np.uint8).reshape(k // 512, 16, n))


def unpack_weight(words, scales, fmt):
    g, _, n = scales.shape
    words = np.ascontiguousarray(words).reshape(g, 128, n, -1)
    if fmt == "e4m3":
        vals = words.view(ml_dtypes.float8_e4m3fn).astype(np.float64)
    else:
        nib = np.empty((g, 128, n, 4), np.uint8)
        nib[..., 0::2] = words & 0xF
        nib[..., 1::2] = words >> 4
        vals = E2M1[nib]
    vals = vals * np.repeat(np.exp2(scales.astype(np.float64) - 127.0), 8, axis=1)[..., None]
    return vals.transpose(0, 1, 3, 2).reshape(g * 512, n)


K, M, T, S = 1536, 128, 4096, 1536


def setup_inputs():
    n = np.random.standard_normal
    s = mx_kscale(K)[:, None]
    v = pack_weight(n((K, T)) * s, "e4m3")
    return {
        "tab_words": v[0],
        "tab_scales": v[1],
        "w": (n((K, M)) / np.sqrt(K) / s).astype(np.float32),
        "ts": np.tile(np.exp(0.5 * n(T)), (128, 1)).astype(np.float32),
        "b": (0.3 * n(128)).astype(np.float32),
        "offs": striped(np.random.permutation(T)[:S]),
    }


def reference(tab_words, tab_scales, w, ts, b, offs):
    tab_ = unpack_weight(tab_words, tab_scales, "e4m3")[:, unstriped(offs)]
    w_ = mxq(f64(w), 0, "e4m3")
    y = w_.T @ tab_
    y = y * f64(ts)[0][unstriped(offs)]
    return y + f64(b)[:, None]

@@ -1,0 +1,156 @@
+from contextlib import ExitStack
+
+import concourse.mybir as mybir
+from concourse.masks import make_identity
+
+K, M, T, S = 1536, 128, 4096, 1536
+FLOPS = 2 * K * M * S
+BYTES = K * T + (K // 32) * T + 4 * K * M + 4 * T + 4 * M + 2 * 128 * (S // 16) + 4 * M * S
+
+F32 = mybir.dt.float32
+BF16 = mybir.dt.bfloat16
+I32 = mybir.dt.int32
+U32 = mybir.dt.uint32
+U16 = mybir.dt.uint16
+U8 = mybir.dt.uint8
+FP8X4 = mybir.dt.float8_e4m3fn_x4
+MULT = mybir.AluOpType.mult
+IDENTITY = mybir.ActivationFunctionType.Identity
+
+P = 128
+PACK = 4
+PASSES = K // (P * PACK)
+N = 512
+SLICES = S // N
+BLOCKS = N // P
+TS_ROW = P - 1
+
+
+def tile_list_tabts_bias_kernel(tc, tab_words, tab_scales, w, ts, b, offs, out):
+    nc = tc.nc
+    with ExitStack() as ctx:
+        keep = ctx.enter_context(tc.tile_pool(name="keep", bufs=1))
+        ring = ctx.enter_context(tc.tile_pool(name="ring", bufs=3))
+        acc_pool = ctx.enter_context(tc.psum_pool(name="acc", bufs=1))
+        flip_pool = ctx.enter_context(tc.psum_pool(name="flip", bufs=2))
+
+        offsets = keep.tile([P, S // 16], U16, name="offsets")
+        nc.sync.dma_start(offsets[:], offs)
+
+        def picks(s):
+            return offsets[:, s * (N // 16) : (s + 1) * (N // 16)]
+
+        ts_window = keep.tile([P, T], F32, name="ts_window")
+        nc.sync.dma_start(ts_window[TS_ROW:P, :], ts[0:1, :])
+        nc.vector.memset(ts_window[0:TS_ROW, :], 0.0)
+
+        bias = keep.tile([P, 1], F32, name="bias")
+        with nc.allow_non_contiguous_dma(reason="one bias value a partition"):
+            nc.sync.dma_start(bias[:], b.rearrange("(p o) -> p o", o=1))
+
+        scale_window = keep.tile([P, T // 4], I32, name="scale_window")
+        nc.vector.memset(scale_window[:], 0)
+        for q in range(4):
+            nc.scalar.dma_start(
+                scale_window[32 * q : 32 * q + 4 * PASSES, :],
+                tab_scales[:, 4 * q : 4 * q + 4, :].bitcast(I32),
+            )
+
+        word_windows = [keep.tile([P, T], I32, name=f"word_window{a}") for a in range(PASSES)]
+
+        def load_words(a):
+            nc.sync.dma_start(word_windows[a][:], tab_words[a].rearrange("p t i -> p (t i)").bitcast(I32))
+
+        w_rows = w.rearrange("(a p i) n -> p a (i n)", p=P, i=PACK)
+        w_bf16 = keep.tile([P, PASSES, M, PACK], BF16, name="w_bf16", align_bytes=64)
+        w_codes = keep.tile([P, PASSES * M], U32, name="w_codes", align_bytes=64)
+        w_scales = keep.tile([P, PASSES * M], U8, name="w_scales", align_bytes=64)
+
+        def load_w(a0, a1):
+            raw = keep.tile([P, a1 - a0, PACK * M], F32, name="w_raw")
+            nc.sync.dma_start(raw[:], w_rows[:, a0:a1, :])
+            for a in range(a0, a1):
+                nc.scalar.copy(w_bf16[:, a, :, :], raw[:, a - a0, :].rearrange("p (i n) -> p n i", i=PACK))
+
+        def quantize_w(a0, a1):
+            nc.vector.quantize_mx(
+                out=w_codes[:, a0 * M : a1 * M].bitcast(FP8X4),
+                scales=w_scales[:, a0 * M : a1 * M],
+                in_=w_bf16[:, a0:a1, :, :].rearrange("p a n i -> p (a n i)"),
+            )
+
+        load_words(0)
+        load_w(0, 2)
+        load_words(1)
+        load_words(2)
+        load_w(2, 3)
+
+        identity = keep.tile([P, P], F32, name="identity")
+        make_identity(nc, identity[:])
+
+        ts_picked = keep.tile([P, S], F32, name="ts_picked")
+        nc.vector.tensor_copy(ts_picked[:], ts_window[:].indirect(offsets[:]))
+        ts_columns = keep.tile([P, SLICES * BLOCKS], F32, name="ts_columns")
+        ts_spread = keep.tile([P, S], F32, name="ts_spread")
+        for s in range(SLICES):
+            turned = flip_pool.tile([P, BLOCKS, P], F32, name="turned")
+            for i in range(BLOCKS):
+                c0 = s * N + i * P
+                nc.tensor.transpose(turned[:, i, :], ts_picked[:, c0 : c0 + P], identity[:])
+            nc.scalar.copy(ts_columns[:, s * BLOCKS : (s + 1) * BLOCKS], turned[:, :, TS_ROW])
+        for s in range(SLICES):
+            spread = flip_pool.tile([P, N], F32, name="spread")
+            for i in range(BLOCKS):
+                c = s * BLOCKS + i
+                nc.tensor.transpose(
+                    spread[:, i * P : (i + 1) * P], ts_columns[:, c : c + 1].to_broadcast([P, P]), identity[:]
+                )
+            nc.scalar.copy(ts_spread[:, s * N : (s + 1) * N], spread[:])
+
+        scales_picked = keep.tile([P, S], U8, name="scales_picked", align_bytes=64)
+        sums = [acc_pool.tile([P, N], F32, name=f"sum{s}") for s in range(SLICES)]
+
+        def gather_words(a, s):
+            picked = ring.tile([P, N], U32, name="words_picked", align_bytes=64)
+            nc.vector.tensor_copy(picked[:], word_windows[a][:].bitcast(U32).indirect(picks(s)))
+            return picked
+
+        def multiply(a, s, picked):
+            nc.tensor.matmul_mx(
+                out=sums[s][:],
+                lhsT=w_codes[:, a * M : (a + 1) * M].bitcast(FP8X4),
+                lhsT_scale=w_scales[:, a * M : (a + 1) * M],
+                rhs=picked[:].bitcast(FP8X4),
+                rhs_scale=scales_picked[4 * a : P, s * N : (s + 1) * N],
+                start=(a == 0),
+                stop=(a == PASSES - 1),
+            )
+
+        scaled = keep.tile([P, S], F32, name="scaled")
+        result = keep.tile([P, S], F32, name="result")
+
+        def finish(s, c0, c1):
+            cols = slice(s * N + c0, s * N + c1)
+            nc.vector.tensor_tensor(scaled[:, cols], sums[s][:, c0:c1], ts_spread[:, cols], MULT)
+            nc.scalar.activation(result[:, cols], scaled[:, cols], IDENTITY, bias=bias[:])
+            nc.sync.dma_start(out[:, cols], result[:, cols])
+
+        first = [gather_words(0, s) for s in range(SLICES)]
+        quantize_w(0, 2)
+        for s in range(SLICES):
+            nc.vector.tensor_copy(
+                scales_picked[:, s * N : (s + 1) * N], scale_window[:].bitcast(U8).indirect(picks(s))
+            )
+            multiply(0, s, first[s])
+        for s in range(SLICES):
+            multiply(1, s, gather_words(1, s))
+
+        picked = gather_words(2, 0)
+        quantize_w(2, 3)
+        multiply(2, 0, picked)
+        multiply(2, 1, gather_words(2, 1))
+        finish(0, 0, N)
+        multiply(2, 2, gather_words(2, 2))
+        finish(1, 0, N)
+        finish(2, 0, N // 2)
+        finish(2, N // 2, N)

@@ -24,12 +24,14 @@ N = 512
 SLICES = S // N
 BLOCKS = N // P
 TS_ROW = P - 1
+TS_SPLIT = 1536
 
 
 def tile_list_tabts_bias_kernel(tc, tab_words, tab_scales, w, ts, b, offs, out):
     nc = tc.nc
     with ExitStack() as ctx:
         keep = ctx.enter_context(tc.tile_pool(name="keep", bufs=1))
+        windows = ctx.enter_context(tc.tile_pool(name="windows", bufs=2))
         ring = ctx.enter_context(tc.tile_pool(name="ring", bufs=3))
         acc_pool = ctx.enter_context(tc.psum_pool(name="acc", bufs=1))
         flip_pool = ctx.enter_context(tc.psum_pool(name="flip", bufs=2))
@@ -40,23 +42,22 @@ def tile_list_tabts_bias_kernel(tc, tab_words, tab_scales, w, ts, b, offs, out):
         def picks(s):
             return offsets[:, s * (N // 16) : (s + 1) * (N // 16)]
 
-        ts_window = keep.tile([P, T], F32, name="ts_window")
+        ts_window = windows.tile([P, T], F32, name="ts_window", tag="window")
         nc.sync.dma_start(ts_window[TS_ROW:P, :], ts[0:1, :])
-        nc.vector.memset(ts_window[0:TS_ROW, :], 0.0)
-
-        bias = keep.tile([P, 1], F32, name="bias")
-        with nc.allow_non_contiguous_dma(reason="one bias value a partition"):
-            nc.sync.dma_start(bias[:], b.rearrange("(p o) -> p o", o=1))
 
         scale_window = keep.tile([P, T // 4], I32, name="scale_window")
-        nc.vector.memset(scale_window[:], 0)
+        for c0, c1 in ((0, T // 4 - 1), (T // 4 - 1, T // 4)):
+            nc.vector.memset(scale_window[:, c0:c1], 0)
+        for c0, c1 in ((0, TS_SPLIT - 1), (TS_SPLIT - 1, TS_SPLIT)):
+            nc.vector.memset(ts_window[0:TS_ROW, c0:c1], 0.0)
+        nc.gpsimd.memset(ts_window[0:TS_ROW, TS_SPLIT:T], 0.0)
         for q in range(4):
-            nc.scalar.dma_start(
+            nc.sync.dma_start(
                 scale_window[32 * q : 32 * q + 4 * PASSES, :],
                 tab_scales[:, 4 * q : 4 * q + 4, :].bitcast(I32),
             )
 
-        word_windows = [keep.tile([P, T], I32, name=f"word_window{a}") for a in range(PASSES)]
+        word_windows = [windows.tile([P, T], I32, name=f"word_window{a}", tag="window") for a in range(PASSES)]
 
         def load_words(a):
             nc.sync.dma_start(word_windows[a][:], tab_words[a].rearrange("p t i -> p (t i)").bitcast(I32))
@@ -80,10 +81,13 @@ def tile_list_tabts_bias_kernel(tc, tab_words, tab_scales, w, ts, b, offs, out):
             )
 
         load_words(0)
-        load_w(0, 2)
+        load_w(0, 3)
+        bias = keep.tile([P, 1], F32, name="bias")
+        with nc.allow_non_contiguous_dma(reason="one bias value a partition"):
+            nc.sync.dma_start(bias[:], b.rearrange("(p o) -> p o", o=1))
+
         load_words(1)
         load_words(2)
-        load_w(2, 3)
 
         identity = keep.tile([P, P], F32, name="identity")
         make_identity(nc, identity[:])
@@ -113,14 +117,14 @@ def tile_list_tabts_bias_kernel(tc, tab_words, tab_scales, w, ts, b, offs, out):
         def gather_words(a, s):
             picked = ring.tile([P, N], U32, name="words_picked", align_bytes=64)
             nc.vector.tensor_copy(picked[:], word_windows[a][:].bitcast(U32).indirect(picks(s)))
-            return picked
+            return picked[:]
 
         def multiply(a, s, picked):
             nc.tensor.matmul_mx(
                 out=sums[s][:],
                 lhsT=w_codes[:, a * M : (a + 1) * M].bitcast(FP8X4),
                 lhsT_scale=w_scales[:, a * M : (a + 1) * M],
-                rhs=picked[:].bitcast(FP8X4),
+                rhs=picked.bitcast(FP8X4),
                 rhs_scale=scales_picked[4 * a : P, s * N : (s + 1) * N],
                 start=(a == 0),
                 stop=(a == PASSES - 1),
@@ -135,22 +139,32 @@ def tile_list_tabts_bias_kernel(tc, tab_words, tab_scales, w, ts, b, offs, out):
             nc.scalar.activation(result[:, cols], scaled[:, cols], IDENTITY, bias=bias[:])
             nc.sync.dma_start(out[:, cols], result[:, cols])
 
-        first = [gather_words(0, s) for s in range(SLICES)]
-        quantize_w(0, 2)
-        for s in range(SLICES):
-            nc.vector.tensor_copy(
-                scales_picked[:, s * N : (s + 1) * N], scale_window[:].bitcast(U8).indirect(picks(s))
-            )
-            multiply(0, s, first[s])
-        for s in range(SLICES):
-            multiply(1, s, gather_words(1, s))
+        def gather_pass(a):
+            picked = keep.tile([P, S], U32, name=f"pass_picked{a}", align_bytes=64)
+            nc.vector.tensor_copy(picked[:], word_windows[a][:].bitcast(U32).indirect(offsets[:]))
+            return picked
 
-        picked = gather_words(2, 0)
+        first = gather_pass(0)
+        quantize_w(0, 2)
         quantize_w(2, 3)
-        multiply(2, 0, picked)
+        nc.vector.tensor_copy(scales_picked[:], scale_window[:].bitcast(U8).indirect(offsets[:]))
+        for s in range(SLICES):
+            multiply(0, s, first[:, s * N : (s + 1) * N])
+        second = gather_pass(1)
+        for s in range(SLICES):
+            multiply(1, s, second[:, s * N : (s + 1) * N])
+
+        multiply(2, 0, gather_words(2, 0))
         multiply(2, 1, gather_words(2, 1))
         finish(0, 0, N)
         multiply(2, 2, gather_words(2, 2))
         finish(1, 0, N)
-        finish(2, 0, N // 2)
-        finish(2, N // 2, N)
+        halves = [(0, N // 2), (N // 2, N)]
+        last = (SLICES - 1) * N
+        for c0, c1 in halves:
+            cols = slice(last + c0, last + c1)
+            nc.vector.tensor_tensor(scaled[:, cols], sums[SLICES - 1][:, c0:c1], ts_spread[:, cols], MULT)
+        for c0, c1 in halves:
+            cols = slice(last + c0, last + c1)
+            nc.vector.tensor_scalar_add(result[:, cols], scaled[:, cols], bias[:])
+        nc.sync.dma_start(out[:, last:S], result[:, last:S])

@@ -31,7 +31,6 @@ def tile_list_tabts_bias_kernel(tc, tab_words, tab_scales, w, ts, b, offs, out):
     nc = tc.nc
     with ExitStack() as ctx:
         keep = ctx.enter_context(tc.tile_pool(name="keep", bufs=1))
-        windows = ctx.enter_context(tc.tile_pool(name="windows", bufs=2))
         ring = ctx.enter_context(tc.tile_pool(name="ring", bufs=3))
         acc_pool = ctx.enter_context(tc.psum_pool(name="acc", bufs=1))
         flip_pool = ctx.enter_context(tc.psum_pool(name="flip", bufs=2))
@@ -42,29 +41,29 @@ def tile_list_tabts_bias_kernel(tc, tab_words, tab_scales, w, ts, b, offs, out):
         def picks(s):
             return offsets[:, s * (N // 16) : (s + 1) * (N // 16)]
 
-        ts_window = windows.tile([P, T], F32, name="ts_window", tag="window")
+        ts_window = keep.tile([P, T], F32, name="ts_window")
         nc.sync.dma_start(ts_window[TS_ROW:P, :], ts[0:1, :])
 
-        scale_window = keep.tile([P, T // 4], I32, name="scale_window")
+        scale_window = keep.tile([P, T // 4], I32, name="scale_window", tag="slot_b", align_bytes=64)
         for c0, c1 in ((0, T // 4 - 1), (T // 4 - 1, T // 4)):
             nc.vector.memset(scale_window[:, c0:c1], 0)
         for c0, c1 in ((0, TS_SPLIT - 1), (TS_SPLIT - 1, TS_SPLIT)):
             nc.vector.memset(ts_window[0:TS_ROW, c0:c1], 0.0)
         nc.gpsimd.memset(ts_window[0:TS_ROW, TS_SPLIT:T], 0.0)
         for q in range(4):
-            nc.sync.dma_start(
+            nc.gpsimd.dma_start(
                 scale_window[32 * q : 32 * q + 4 * PASSES, :],
                 tab_scales[:, 4 * q : 4 * q + 4, :].bitcast(I32),
             )
 
-        word_windows = [windows.tile([P, T], I32, name=f"word_window{a}", tag="window") for a in range(PASSES)]
+        word_windows = [keep.tile([P, T], I32, name=f"word_window{a}", tag=f"window{a}", align_bytes=64) for a in range(PASSES)]
 
         def load_words(a):
             nc.sync.dma_start(word_windows[a][:], tab_words[a].rearrange("p t i -> p (t i)").bitcast(I32))
 
         w_rows = w.rearrange("(a p i) n -> p a (i n)", p=P, i=PACK)
-        w_bf16 = keep.tile([P, PASSES, M, PACK], BF16, name="w_bf16", align_bytes=64)
-        w_codes = keep.tile([P, PASSES * M], U32, name="w_codes", align_bytes=64)
+        w_bf16 = keep.tile([P, PASSES, M, PACK], BF16, name="w_bf16", tag="picked1", align_bytes=64)
+        w_codes = keep.tile([P, PASSES * M], U32, name="w_codes", tag="slot_b", align_bytes=64)
         w_scales = keep.tile([P, PASSES * M], U8, name="w_scales", align_bytes=64)
 
         def load_w(a0, a1):
@@ -111,7 +110,7 @@ def tile_list_tabts_bias_kernel(tc, tab_words, tab_scales, w, ts, b, offs, out):
                 )
             nc.scalar.copy(ts_spread[:, s * N : (s + 1) * N], spread[:])
 
-        scales_picked = keep.tile([P, S], U8, name="scales_picked", align_bytes=64)
+        scales_picked = keep.tile([P, S], U8, name="scales_picked", tag="window0", align_bytes=64)
         sums = [acc_pool.tile([P, N], F32, name=f"sum{s}") for s in range(SLICES)]
 
         def gather_words(a, s):
@@ -140,14 +139,14 @@ def tile_list_tabts_bias_kernel(tc, tab_words, tab_scales, w, ts, b, offs, out):
             nc.sync.dma_start(out[:, cols], result[:, cols])
 
         def gather_pass(a):
-            picked = keep.tile([P, S], U32, name=f"pass_picked{a}", align_bytes=64)
+            picked = keep.tile([P, S], U32, name=f"pass_picked{a}", tag=f"picked{a}", align_bytes=64)
             nc.vector.tensor_copy(picked[:], word_windows[a][:].bitcast(U32).indirect(offsets[:]))
             return picked
 
         first = gather_pass(0)
+        nc.vector.tensor_copy(scales_picked[:], scale_window[:].bitcast(U8).indirect(offsets[:]))
         quantize_w(0, 2)
         quantize_w(2, 3)
-        nc.vector.tensor_copy(scales_picked[:], scale_window[:].bitcast(U8).indirect(offsets[:]))
         for s in range(SLICES):
             multiply(0, s, first[:, s * N : (s + 1) * N])
         second = gather_pass(1)

@@ -23,7 +23,7 @@ PASSES = K // (P * PACK)
 N = 512
 SLICES = S // N
 BLOCKS = N // P
-TS_ROW = P - 1
+LIVE_ROW = P - 1
 TS_SPLIT = 1536
 
 
@@ -31,76 +31,73 @@ def tile_list_tabts_bias_kernel(tc, tab_words, tab_scales, w, ts, b, offs, out):
     nc = tc.nc
     with ExitStack() as ctx:
         keep = ctx.enter_context(tc.tile_pool(name="keep", bufs=1))
-        ring = ctx.enter_context(tc.tile_pool(name="ring", bufs=3))
         acc_pool = ctx.enter_context(tc.psum_pool(name="acc", bufs=1))
         flip_pool = ctx.enter_context(tc.psum_pool(name="flip", bufs=2))
+
+        def tile(shape, dtype, name, slot=None):
+            return keep.tile(shape, dtype, name=name, tag=slot or name, align_bytes=64)
 
         offsets = keep.tile([P, S // 16], U16, name="offsets")
         nc.sync.dma_start(offsets[:], offs)
 
-        def picks(s):
-            return offsets[:, s * (N // 16) : (s + 1) * (N // 16)]
+        ts_window = tile([P, T], F32, "ts_window", "slot_ts_words1")
+        nc.sync.dma_start(ts_window[LIVE_ROW:P, :], ts[0:1, :])
 
-        ts_window = keep.tile([P, T], F32, name="ts_window")
-        nc.sync.dma_start(ts_window[TS_ROW:P, :], ts[0:1, :])
-
-        scale_window = keep.tile([P, T // 4], I32, name="scale_window", tag="slot_b", align_bytes=64)
+        scale_window = tile([P, T // 4], I32, "scale_window", "slot_scales_w")
         for c0, c1 in ((0, T // 4 - 1), (T // 4 - 1, T // 4)):
             nc.vector.memset(scale_window[:, c0:c1], 0)
         for c0, c1 in ((0, TS_SPLIT - 1), (TS_SPLIT - 1, TS_SPLIT)):
-            nc.vector.memset(ts_window[0:TS_ROW, c0:c1], 0.0)
-        nc.gpsimd.memset(ts_window[0:TS_ROW, TS_SPLIT:T], 0.0)
+            nc.vector.memset(ts_window[0:LIVE_ROW, c0:c1], 0.0)
+        nc.gpsimd.memset(ts_window[0:LIVE_ROW, TS_SPLIT:T], 0.0)
+
+        def load_words(a, slot):
+            window = tile([P, T], I32, f"word_window{a}", slot)
+            nc.sync.dma_start(window[:], tab_words[a].rearrange("p t i -> p (t i)").bitcast(I32))
+            return window
+
+        w_rows = w.rearrange("(a p i) n -> p a (i n)", p=P, i=PACK)
+        w_bf16 = tile([P, PASSES, M, PACK], BF16, "w_bf16")
+
+        def load_w(a, raw):
+            nc.sync.dma_start(raw, w_rows[:, a, :])
+            nc.scalar.copy(w_bf16[:, a, :, :], raw.rearrange("p (i n) -> p n i", i=PACK))
+
+        window0 = load_words(0, "slot_words0_scales")
+        w_first = tile([P, PACK * M], F32, "w_first")
+        load_w(0, w_first[:])
+
+        bias_row = tile([P, P], F32, "bias_row")
+        nc.sync.dma_start(bias_row[LIVE_ROW:P, :], b.rearrange("(o n) -> o n", o=1))
+        nc.gpsimd.memset(bias_row[0:LIVE_ROW, :], 0.0)
+
         for q in range(4):
-            nc.gpsimd.dma_start(
+            nc.sync.dma_start(
                 scale_window[32 * q : 32 * q + 4 * PASSES, :],
                 tab_scales[:, 4 * q : 4 * q + 4, :].bitcast(I32),
             )
 
-        word_windows = [keep.tile([P, T], I32, name=f"word_window{a}", tag=f"window{a}", align_bytes=64) for a in range(PASSES)]
-
-        def load_words(a):
-            nc.sync.dma_start(word_windows[a][:], tab_words[a].rearrange("p t i -> p (t i)").bitcast(I32))
-
-        w_rows = w.rearrange("(a p i) n -> p a (i n)", p=P, i=PACK)
-        w_bf16 = keep.tile([P, PASSES, M, PACK], BF16, name="w_bf16", tag="picked1", align_bytes=64)
-        w_codes = keep.tile([P, PASSES * M], U32, name="w_codes", tag="slot_b", align_bytes=64)
-        w_scales = keep.tile([P, PASSES * M], U8, name="w_scales", align_bytes=64)
-
-        def load_w(a0, a1):
-            raw = keep.tile([P, a1 - a0, PACK * M], F32, name="w_raw")
-            nc.sync.dma_start(raw[:], w_rows[:, a0:a1, :])
-            for a in range(a0, a1):
-                nc.scalar.copy(w_bf16[:, a, :, :], raw[:, a - a0, :].rearrange("p (i n) -> p n i", i=PACK))
-
-        def quantize_w(a0, a1):
-            nc.vector.quantize_mx(
-                out=w_codes[:, a0 * M : a1 * M].bitcast(FP8X4),
-                scales=w_scales[:, a0 * M : a1 * M],
-                in_=w_bf16[:, a0:a1, :, :].rearrange("p a n i -> p (a n i)"),
-            )
-
-        load_words(0)
-        load_w(0, 3)
-        bias = keep.tile([P, 1], F32, name="bias")
-        with nc.allow_non_contiguous_dma(reason="one bias value a partition"):
-            nc.sync.dma_start(bias[:], b.rearrange("(p o) -> p o", o=1))
-
-        load_words(1)
-        load_words(2)
-
-        identity = keep.tile([P, P], F32, name="identity")
+        identity = tile([P, P], F32, "identity")
         make_identity(nc, identity[:])
 
-        ts_picked = keep.tile([P, S], F32, name="ts_picked")
+        ts_picked = tile([P, S], F32, "ts_picked", "slot_picked_words2")
         nc.vector.tensor_copy(ts_picked[:], ts_window[:].indirect(offsets[:]))
-        ts_columns = keep.tile([P, SLICES * BLOCKS], F32, name="ts_columns")
-        ts_spread = keep.tile([P, S], F32, name="ts_spread")
+        window1 = load_words(1, "slot_ts_words1")
+
+        ts_columns = tile([P, SLICES * BLOCKS], F32, "ts_columns")
+        ts_spread = tile([P, S], F32, "ts_spread")
         for s in range(SLICES):
             turned = flip_pool.tile([P, BLOCKS, P], F32, name="turned")
             for i in range(BLOCKS):
                 c0 = s * N + i * P
                 nc.tensor.transpose(turned[:, i, :], ts_picked[:, c0 : c0 + P], identity[:])
-            nc.scalar.copy(ts_columns[:, s * BLOCKS : (s + 1) * BLOCKS], turned[:, :, TS_ROW])
+            nc.scalar.copy(ts_columns[:, s * BLOCKS : (s + 1) * BLOCKS], turned[:, :, LIVE_ROW])
+        window2 = load_words(2, "slot_picked_words2")
+
+        bias = tile([P, 1], F32, "bias")
+        turned = flip_pool.tile([P, BLOCKS, P], F32, name="turned")
+        nc.tensor.transpose(turned[:, 0, :], bias_row[:], identity[:])
+        nc.scalar.copy(bias[:], turned[:, 0, LIVE_ROW:P])
+
         for s in range(SLICES):
             spread = flip_pool.tile([P, N], F32, name="spread")
             for i in range(BLOCKS):
@@ -110,56 +107,69 @@ def tile_list_tabts_bias_kernel(tc, tab_words, tab_scales, w, ts, b, offs, out):
                 )
             nc.scalar.copy(ts_spread[:, s * N : (s + 1) * N], spread[:])
 
-        scales_picked = keep.tile([P, S], U8, name="scales_picked", tag="window0", align_bytes=64)
+        picked = [tile([P, S], U32, f"picked{a}") for a in range(PASSES)]
+        nc.vector.tensor_copy(picked[0][:], window0[:].bitcast(U32).indirect(offsets[:]))
+        scales_picked = tile([P, S], U8, "scales_picked", "slot_words0_scales")
+        nc.vector.tensor_copy(scales_picked[:], scale_window[:].bitcast(U8).indirect(offsets[:]))
+
+        w_rest = tile([P, PASSES - 1, PACK * M], F32, "w_rest", "slot_scales_w")
+        for a in range(1, PASSES):
+            load_w(a, w_rest[:, a - 1, :])
+
+        nc.vector.tensor_copy(picked[1][:], window1[:].bitcast(U32).indirect(offsets[:]))
+
+        w_codes = tile([P, PASSES * M], U32, "w_codes", "slot_ts_words1")
+        w_scales = tile([P, PASSES * M], U8, "w_scales")
         sums = [acc_pool.tile([P, N], F32, name=f"sum{s}") for s in range(SLICES)]
 
-        def gather_words(a, s):
-            picked = ring.tile([P, N], U32, name="words_picked", align_bytes=64)
-            nc.vector.tensor_copy(picked[:], word_windows[a][:].bitcast(U32).indirect(picks(s)))
-            return picked[:]
+        def quantize_w(a):
+            nc.vector.quantize_mx(
+                out=w_codes[:, a * M : (a + 1) * M].bitcast(FP8X4),
+                scales=w_scales[:, a * M : (a + 1) * M],
+                in_=w_bf16[:, a, :, :].rearrange("p n i -> p (n i)"),
+            )
 
-        def multiply(a, s, picked):
+        def multiply(a, s):
+            cols = slice(s * N, (s + 1) * N)
             nc.tensor.matmul_mx(
                 out=sums[s][:],
                 lhsT=w_codes[:, a * M : (a + 1) * M].bitcast(FP8X4),
                 lhsT_scale=w_scales[:, a * M : (a + 1) * M],
-                rhs=picked.bitcast(FP8X4),
-                rhs_scale=scales_picked[4 * a : P, s * N : (s + 1) * N],
+                rhs=picked[a][:, cols].bitcast(FP8X4),
+                rhs_scale=scales_picked[4 * a : P, cols],
                 start=(a == 0),
                 stop=(a == PASSES - 1),
             )
 
-        scaled = keep.tile([P, S], F32, name="scaled")
-        result = keep.tile([P, S], F32, name="result")
+        def gather_last(s):
+            nc.vector.tensor_copy(
+                picked[2][:, s * N : (s + 1) * N],
+                window2[:].bitcast(U32).indirect(offsets[:, s * (N // 16) : (s + 1) * (N // 16)]),
+            )
 
-        def finish(s, c0, c1):
-            cols = slice(s * N + c0, s * N + c1)
-            nc.vector.tensor_tensor(scaled[:, cols], sums[s][:, c0:c1], ts_spread[:, cols], MULT)
+        quantize_w(0)
+        for s in range(SLICES):
+            multiply(0, s)
+        gather_last(0)
+        quantize_w(1)
+        for s in range(SLICES):
+            multiply(1, s)
+        gather_last(1)
+        quantize_w(2)
+        multiply(2, 0)
+        multiply(2, 1)
+        gather_last(2)
+        multiply(2, 2)
+
+        scaled = tile([P, S], F32, "scaled")
+        result = tile([P, S], F32, "result")
+        for s in range(SLICES - 1):
+            cols = slice(s * N, (s + 1) * N)
+            nc.vector.tensor_tensor(scaled[:, cols], sums[s][:], ts_spread[:, cols], MULT)
             nc.scalar.activation(result[:, cols], scaled[:, cols], IDENTITY, bias=bias[:])
             nc.sync.dma_start(out[:, cols], result[:, cols])
-
-        def gather_pass(a):
-            picked = keep.tile([P, S], U32, name=f"pass_picked{a}", tag=f"picked{a}", align_bytes=64)
-            nc.vector.tensor_copy(picked[:], word_windows[a][:].bitcast(U32).indirect(offsets[:]))
-            return picked
-
-        first = gather_pass(0)
-        nc.vector.tensor_copy(scales_picked[:], scale_window[:].bitcast(U8).indirect(offsets[:]))
-        quantize_w(0, 2)
-        quantize_w(2, 3)
-        for s in range(SLICES):
-            multiply(0, s, first[:, s * N : (s + 1) * N])
-        second = gather_pass(1)
-        for s in range(SLICES):
-            multiply(1, s, second[:, s * N : (s + 1) * N])
-
-        multiply(2, 0, gather_words(2, 0))
-        multiply(2, 1, gather_words(2, 1))
-        finish(0, 0, N)
-        multiply(2, 2, gather_words(2, 2))
-        finish(1, 0, N)
-        halves = [(0, N // 2), (N // 2, N)]
         last = (SLICES - 1) * N
+        halves = [(0, N // 2), (N // 2, N)]
         for c0, c1 in halves:
             cols = slice(last + c0, last + c1)
             nc.vector.tensor_tensor(scaled[:, cols], sums[SLICES - 1][:, c0:c1], ts_spread[:, cols], MULT)

@@ -56,19 +56,19 @@ def tile_list_tabts_bias_kernel(tc, tab_words, tab_scales, w, ts, b, offs, out):
             return window
 
         w_rows = w.rearrange("(a p i) n -> p a (i n)", p=P, i=PACK)
-        w_bf16 = tile([P, PASSES, M, PACK], BF16, "w_bf16")
+        w_bf16 = [tile([P, M, PACK], BF16, f"w_bf16_{a}", f"slot_w_last{a}") for a in range(PASSES)]
 
         def load_w(a, raw):
             nc.sync.dma_start(raw, w_rows[:, a, :])
-            nc.scalar.copy(w_bf16[:, a, :, :], raw.rearrange("p (i n) -> p n i", i=PACK))
-
-        window0 = load_words(0, "slot_words0_scales")
-        w_first = tile([P, PACK * M], F32, "w_first")
-        load_w(0, w_first[:])
+            nc.scalar.copy(w_bf16[a][:], raw.rearrange("p (i n) -> p n i", i=PACK))
 
         bias_row = tile([P, P], F32, "bias_row")
         nc.sync.dma_start(bias_row[LIVE_ROW:P, :], b.rearrange("(o n) -> o n", o=1))
         nc.gpsimd.memset(bias_row[0:LIVE_ROW, :], 0.0)
+
+        window0 = load_words(0, "slot_words0_scales")
+        w_first = tile([P, PACK * M], F32, "w_first")
+        load_w(0, w_first[:])
 
         for q in range(4):
             nc.sync.dma_start(
@@ -107,7 +107,7 @@ def tile_list_tabts_bias_kernel(tc, tab_words, tab_scales, w, ts, b, offs, out):
                 )
             nc.scalar.copy(ts_spread[:, s * N : (s + 1) * N], spread[:])
 
-        picked = [tile([P, S], U32, f"picked{a}") for a in range(PASSES)]
+        picked = [tile([P, S], U32, f"picked{a}") for a in range(PASSES - 1)]
         nc.vector.tensor_copy(picked[0][:], window0[:].bitcast(U32).indirect(offsets[:]))
         scales_picked = tile([P, S], U8, "scales_picked", "slot_words0_scales")
         nc.vector.tensor_copy(scales_picked[:], scale_window[:].bitcast(U8).indirect(offsets[:]))
@@ -126,40 +126,40 @@ def tile_list_tabts_bias_kernel(tc, tab_words, tab_scales, w, ts, b, offs, out):
             nc.vector.quantize_mx(
                 out=w_codes[:, a * M : (a + 1) * M].bitcast(FP8X4),
                 scales=w_scales[:, a * M : (a + 1) * M],
-                in_=w_bf16[:, a, :, :].rearrange("p n i -> p (n i)"),
+                in_=w_bf16[a][:].rearrange("p n i -> p (n i)"),
             )
 
-        def multiply(a, s):
+        def multiply(a, s, words):
             cols = slice(s * N, (s + 1) * N)
             nc.tensor.matmul_mx(
                 out=sums[s][:],
                 lhsT=w_codes[:, a * M : (a + 1) * M].bitcast(FP8X4),
                 lhsT_scale=w_scales[:, a * M : (a + 1) * M],
-                rhs=picked[a][:, cols].bitcast(FP8X4),
+                rhs=words.bitcast(FP8X4),
                 rhs_scale=scales_picked[4 * a : P, cols],
                 start=(a == 0),
                 stop=(a == PASSES - 1),
             )
 
         def gather_last(s):
+            words = tile([P, N], U32, f"picked_last{s}", f"slot_w_last{s}")
             nc.vector.tensor_copy(
-                picked[2][:, s * N : (s + 1) * N],
-                window2[:].bitcast(U32).indirect(offsets[:, s * (N // 16) : (s + 1) * (N // 16)]),
+                words[:], window2[:].bitcast(U32).indirect(offsets[:, s * (N // 16) : (s + 1) * (N // 16)])
             )
+            return words[:]
 
         quantize_w(0)
         for s in range(SLICES):
-            multiply(0, s)
-        gather_last(0)
+            multiply(0, s, picked[0][:, s * N : (s + 1) * N])
+        last0 = gather_last(0)
         quantize_w(1)
         for s in range(SLICES):
-            multiply(1, s)
-        gather_last(1)
+            multiply(1, s, picked[1][:, s * N : (s + 1) * N])
+        last1 = gather_last(1)
         quantize_w(2)
-        multiply(2, 0)
-        multiply(2, 1)
-        gather_last(2)
-        multiply(2, 2)
+        multiply(2, 0, last0)
+        multiply(2, 1, last1)
+        multiply(2, 2, gather_last(2))
 
         scaled = tile([P, S], F32, "scaled")
         result = tile([P, S], F32, "result")

@@ -24,13 +24,16 @@ N = 512
 SLICES = S // N
 BLOCKS = N // P
 LIVE_ROW = P - 1
-TS_SPLIT = 1536
+TS_SPLIT = 512
+SCALE_BASE = (48, 96, 112)
+EARLY_MOVES = 6
 
 
 def tile_list_tabts_bias_kernel(tc, tab_words, tab_scales, w, ts, b, offs, out):
     nc = tc.nc
     with ExitStack() as ctx:
         keep = ctx.enter_context(tc.tile_pool(name="keep", bufs=1))
+        late = ctx.enter_context(tc.tile_pool(name="late", bufs=1))
         acc_pool = ctx.enter_context(tc.psum_pool(name="acc", bufs=1))
         flip_pool = ctx.enter_context(tc.psum_pool(name="flip", bufs=2))
 
@@ -40,18 +43,28 @@ def tile_list_tabts_bias_kernel(tc, tab_words, tab_scales, w, ts, b, offs, out):
         offsets = keep.tile([P, S // 16], U16, name="offsets")
         nc.sync.dma_start(offsets[:], offs)
 
-        ts_window = tile([P, T], F32, "ts_window", "slot_ts_words1")
-        nc.sync.dma_start(ts_window[LIVE_ROW:P, :], ts[0:1, :])
+        scale_rows = tab_scales.rearrange("a q t -> (a q) t").bitcast(I32)
+        scale_window = late.tile([P, T // 4], I32, name="scale_window", offset=4 * T - 1024)
+        nc.sync.dma_start(scale_window[SCALE_BASE[0] : SCALE_BASE[0] + 16, :], scale_rows[0:16, :])
+        nc.sync.dma_start(scale_window[SCALE_BASE[1] : P, :], scale_rows[16:48, :])
+        for p0, p1 in ((0, SCALE_BASE[0]), (64, SCALE_BASE[1])):
+            for c0, c1 in ((0, T // 4 - 1), (T // 4 - 1, T // 4)):
+                nc.vector.memset(scale_window[p0:p1, c0:c1], 0)
 
-        scale_window = tile([P, T // 4], I32, "scale_window", "slot_scales_w")
-        for c0, c1 in ((0, T // 4 - 1), (T // 4 - 1, T // 4)):
-            nc.vector.memset(scale_window[:, c0:c1], 0)
+        planes = tile([P, PASSES * S // 4], I32, "planes")
+        nc.gpsimd.memset(planes[:], 0)
+
+        ts_window = tile([P, T], F32, "ts_window", "slot_ts_picked0")
+        nc.sync.dma_start(ts_window[LIVE_ROW:P, :], ts[0:1, :])
         for c0, c1 in ((0, TS_SPLIT - 1), (TS_SPLIT - 1, TS_SPLIT)):
             nc.vector.memset(ts_window[0:LIVE_ROW, c0:c1], 0.0)
         nc.gpsimd.memset(ts_window[0:LIVE_ROW, TS_SPLIT:T], 0.0)
 
-        def load_words(a, slot):
-            window = tile([P, T], I32, f"word_window{a}", slot)
+        bias_row = tile([P, P], F32, "bias_row")
+        nc.sync.dma_start(bias_row[LIVE_ROW:P, :], b.rearrange("(o n) -> o n", o=1))
+        nc.gpsimd.memset(bias_row[0:LIVE_ROW, :], 0.0)
+
+        def load_words(a, window):
             nc.sync.dma_start(window[:], tab_words[a].rearrange("p t i -> p (t i)").bitcast(I32))
             return window
 
@@ -59,29 +72,38 @@ def tile_list_tabts_bias_kernel(tc, tab_words, tab_scales, w, ts, b, offs, out):
         w_bf16 = [tile([P, M, PACK], BF16, f"w_bf16_{a}", f"slot_w_last{a}") for a in range(PASSES)]
 
         def load_w(a, raw):
-            nc.sync.dma_start(raw, w_rows[:, a, :])
-            nc.scalar.copy(w_bf16[a][:], raw.rearrange("p (i n) -> p n i", i=PACK))
+            nc.sync.dma_start(raw[:], w_rows[:, a, :])
+            nc.scalar.copy(w_bf16[a][:], raw[:].rearrange("p (i n) -> p n i", i=PACK))
 
-        bias_row = tile([P, P], F32, "bias_row")
-        nc.sync.dma_start(bias_row[LIVE_ROW:P, :], b.rearrange("(o n) -> o n", o=1))
-        nc.gpsimd.memset(bias_row[0:LIVE_ROW, :], 0.0)
-
-        window0 = load_words(0, "slot_words0_scales")
-        w_first = tile([P, PACK * M], F32, "w_first")
-        load_w(0, w_first[:])
-
-        for q in range(4):
-            nc.sync.dma_start(
-                scale_window[32 * q : 32 * q + 4 * PASSES, :],
-                tab_scales[:, 4 * q : 4 * q + 4, :].bitcast(I32),
-            )
+        window0 = load_words(0, tile([P, T], I32, "word_window0"))
+        load_w(0, tile([P, PACK * M], F32, "w_raw0"))
+        window1 = load_words(1, tile([P, T], I32, "word_window1"))
 
         identity = tile([P, P], F32, "identity")
         make_identity(nc, identity[:])
 
-        ts_picked = tile([P, S], F32, "ts_picked", "slot_picked_words2")
+        scales_picked = tile([P, S], U8, "scales_picked")
+        nc.vector.tensor_copy(scales_picked[:], scale_window[:].bitcast(U8).indirect(offsets[:]))
+
+        def place_scales(i):
+            a, q = divmod(i, 4)
+            src = SCALE_BASE[a] + 4 * q
+            dst = 32 * q + 4 * a
+            nc.sync.dma_start(
+                planes[dst : dst + 4, a * (S // 4) : (a + 1) * (S // 4)],
+                scales_picked[src : src + 4, :].bitcast(I32),
+            )
+
+        for i in range(EARLY_MOVES):
+            place_scales(i)
+        window2 = load_words(2, late.tile([P, T], I32, name="word_window2", offset=0))
+        for a in range(1, PASSES):
+            load_w(a, late.tile([P, PACK * M], F32, name=f"w_raw{a}", offset=4 * T + (a - 1) * 4 * PACK * M))
+        for i in range(EARLY_MOVES, 4 * PASSES):
+            place_scales(i)
+
+        ts_picked = tile([P, S], F32, "ts_picked")
         nc.vector.tensor_copy(ts_picked[:], ts_window[:].indirect(offsets[:]))
-        window1 = load_words(1, "slot_ts_words1")
 
         ts_columns = tile([P, SLICES * BLOCKS], F32, "ts_columns")
         ts_spread = tile([P, S], F32, "ts_spread")
@@ -91,7 +113,6 @@ def tile_list_tabts_bias_kernel(tc, tab_words, tab_scales, w, ts, b, offs, out):
                 c0 = s * N + i * P
                 nc.tensor.transpose(turned[:, i, :], ts_picked[:, c0 : c0 + P], identity[:])
             nc.scalar.copy(ts_columns[:, s * BLOCKS : (s + 1) * BLOCKS], turned[:, :, LIVE_ROW])
-        window2 = load_words(2, "slot_picked_words2")
 
         bias = tile([P, 1], F32, "bias")
         turned = flip_pool.tile([P, BLOCKS, P], F32, name="turned")
@@ -107,20 +128,14 @@ def tile_list_tabts_bias_kernel(tc, tab_words, tab_scales, w, ts, b, offs, out):
                 )
             nc.scalar.copy(ts_spread[:, s * N : (s + 1) * N], spread[:])
 
-        picked = [tile([P, S], U32, f"picked{a}") for a in range(PASSES - 1)]
+        picked = [tile([P, S], U32, "picked0", "slot_ts_picked0"), tile([P, S], U32, "picked1")]
         nc.vector.tensor_copy(picked[0][:], window0[:].bitcast(U32).indirect(offsets[:]))
-        scales_picked = tile([P, S], U8, "scales_picked", "slot_words0_scales")
-        nc.vector.tensor_copy(scales_picked[:], scale_window[:].bitcast(U8).indirect(offsets[:]))
-
-        w_rest = tile([P, PASSES - 1, PACK * M], F32, "w_rest", "slot_scales_w")
-        for a in range(1, PASSES):
-            load_w(a, w_rest[:, a - 1, :])
-
         nc.vector.tensor_copy(picked[1][:], window1[:].bitcast(U32).indirect(offsets[:]))
 
-        w_codes = tile([P, PASSES * M], U32, "w_codes", "slot_ts_words1")
+        w_codes = tile([P, PASSES * M], U32, "w_codes")
         w_scales = tile([P, PASSES * M], U8, "w_scales")
-        sums = [acc_pool.tile([P, N], F32, name=f"sum{s}") for s in range(SLICES)]
+        ranges = [(0, N), (N, 2 * N), (2 * N, 2 * N + N // 2), (2 * N + N // 2, S)]
+        sums = [acc_pool.tile([P, c1 - c0], F32, name=f"sum{r}") for r, (c0, c1) in enumerate(ranges)]
 
         def quantize_w(a):
             nc.vector.quantize_mx(
@@ -129,14 +144,14 @@ def tile_list_tabts_bias_kernel(tc, tab_words, tab_scales, w, ts, b, offs, out):
                 in_=w_bf16[a][:].rearrange("p n i -> p (n i)"),
             )
 
-        def multiply(a, s, words):
-            cols = slice(s * N, (s + 1) * N)
+        def multiply(a, r, words, first):
+            c0, c1 = ranges[r]
             nc.tensor.matmul_mx(
-                out=sums[s][:],
+                out=sums[r][:],
                 lhsT=w_codes[:, a * M : (a + 1) * M].bitcast(FP8X4),
                 lhsT_scale=w_scales[:, a * M : (a + 1) * M],
-                rhs=words.bitcast(FP8X4),
-                rhs_scale=scales_picked[4 * a : P, cols],
+                rhs=words[:, c0 - first : c1 - first].bitcast(FP8X4),
+                rhs_scale=planes[4 * a : P, (a * S + c0) // 4 : (a * S + c1) // 4].bitcast(U8),
                 start=(a == 0),
                 stop=(a == PASSES - 1),
             )
@@ -146,34 +161,31 @@ def tile_list_tabts_bias_kernel(tc, tab_words, tab_scales, w, ts, b, offs, out):
             nc.vector.tensor_copy(
                 words[:], window2[:].bitcast(U32).indirect(offsets[:, s * (N // 16) : (s + 1) * (N // 16)])
             )
-            return words[:]
+            return words
 
         quantize_w(0)
-        for s in range(SLICES):
-            multiply(0, s, picked[0][:, s * N : (s + 1) * N])
+        for r in range(len(ranges)):
+            multiply(0, r, picked[0], 0)
         last0 = gather_last(0)
         quantize_w(1)
-        for s in range(SLICES):
-            multiply(1, s, picked[1][:, s * N : (s + 1) * N])
+        for r in range(len(ranges)):
+            multiply(1, r, picked[1], 0)
         last1 = gather_last(1)
         quantize_w(2)
-        multiply(2, 0, last0)
-        multiply(2, 1, last1)
-        multiply(2, 2, gather_last(2))
+        multiply(2, 0, last0, 0)
+        multiply(2, 1, last1, N)
+        last2 = gather_last(2)
+        multiply(2, 2, last2, 2 * N)
+        multiply(2, 3, last2, 2 * N)
 
         scaled = tile([P, S], F32, "scaled")
         result = tile([P, S], F32, "result")
-        for s in range(SLICES - 1):
-            cols = slice(s * N, (s + 1) * N)
-            nc.vector.tensor_tensor(scaled[:, cols], sums[s][:], ts_spread[:, cols], MULT)
-            nc.scalar.activation(result[:, cols], scaled[:, cols], IDENTITY, bias=bias[:])
-            nc.sync.dma_start(out[:, cols], result[:, cols])
-        last = (SLICES - 1) * N
-        halves = [(0, N // 2), (N // 2, N)]
-        for c0, c1 in halves:
-            cols = slice(last + c0, last + c1)
-            nc.vector.tensor_tensor(scaled[:, cols], sums[SLICES - 1][:, c0:c1], ts_spread[:, cols], MULT)
-        for c0, c1 in halves:
-            cols = slice(last + c0, last + c1)
-            nc.vector.tensor_scalar_add(result[:, cols], scaled[:, cols], bias[:])
-        nc.sync.dma_start(out[:, last:S], result[:, last:S])
+        for r, (c0, c1) in enumerate(ranges):
+            nc.vector.tensor_tensor(scaled[:, c0:c1], sums[r][:], ts_spread[:, c0:c1], MULT)
+            if r < len(ranges) - 1:
+                nc.scalar.activation(result[:, c0:c1], scaled[:, c0:c1], IDENTITY, bias=bias[:])
+            else:
+                nc.vector.tensor_scalar_add(result[:, c0:c1], scaled[:, c0:c1], bias[:])
+            if r < 2:
+                nc.sync.dma_start(out[:, c0:c1], result[:, c0:c1])
+        nc.sync.dma_start(out[:, 2 * N : S], result[:, 2 * N : S])

@@ -24,7 +24,6 @@ N = 512
 SLICES = S // N
 BLOCKS = N // P
 LIVE_ROW = P - 1
-TS_SPLIT = 512
 SCALE_BASE = (48, 96, 112)
 EARLY_MOVES = 6
 
@@ -56,9 +55,7 @@ def tile_list_tabts_bias_kernel(tc, tab_words, tab_scales, w, ts, b, offs, out):
 
         ts_window = tile([P, T], F32, "ts_window", "slot_ts_picked0")
         nc.sync.dma_start(ts_window[LIVE_ROW:P, :], ts[0:1, :])
-        for c0, c1 in ((0, TS_SPLIT - 1), (TS_SPLIT - 1, TS_SPLIT)):
-            nc.vector.memset(ts_window[0:LIVE_ROW, c0:c1], 0.0)
-        nc.gpsimd.memset(ts_window[0:LIVE_ROW, TS_SPLIT:T], 0.0)
+        nc.gpsimd.memset(ts_window[0:LIVE_ROW, :], 0.0)
 
         bias_row = tile([P, P], F32, "bias_row")
         nc.sync.dma_start(bias_row[LIVE_ROW:P, :], b.rearrange("(o n) -> o n", o=1))
@@ -186,6 +183,4 @@ def tile_list_tabts_bias_kernel(tc, tab_words, tab_scales, w, ts, b, offs, out):
                 nc.scalar.activation(result[:, c0:c1], scaled[:, c0:c1], IDENTITY, bias=bias[:])
             else:
                 nc.vector.tensor_scalar_add(result[:, c0:c1], scaled[:, c0:c1], bias[:])
-            if r < 2:
-                nc.sync.dma_start(out[:, c0:c1], result[:, c0:c1])
-        nc.sync.dma_start(out[:, 2 * N : S], result[:, 2 * N : S])
+            nc.sync.dma_start(out[:, c0:c1], result[:, c0:c1])

@@ -44,7 +44,7 @@ def tile_list_tabts_bias_kernel(tc, tab_words, tab_scales, w, ts, b, offs, out):
 
         scale_rows = tab_scales.rearrange("a q t -> (a q) t").bitcast(I32)
         scale_window = late.tile([P, T // 4], I32, name="scale_window", offset=4 * T - 1024)
-        nc.sync.dma_start(scale_window[SCALE_BASE[0] : SCALE_BASE[0] + 16, :], scale_rows[0:16, :])
+        nc.scalar.dma_start(scale_window[SCALE_BASE[0] : SCALE_BASE[0] + 16, :], scale_rows[0:16, :])
         nc.sync.dma_start(scale_window[SCALE_BASE[1] : P, :], scale_rows[16:48, :])
         for p0, p1 in ((0, SCALE_BASE[0]), (64, SCALE_BASE[1])):
             for c0, c1 in ((0, T // 4 - 1), (T // 4 - 1, T // 4)):
@@ -54,11 +54,11 @@ def tile_list_tabts_bias_kernel(tc, tab_words, tab_scales, w, ts, b, offs, out):
         nc.gpsimd.memset(planes[:], 0)
 
         ts_window = tile([P, T], F32, "ts_window", "slot_ts_picked0")
-        nc.sync.dma_start(ts_window[LIVE_ROW:P, :], ts[0:1, :])
+        nc.scalar.dma_start(ts_window[LIVE_ROW:P, :], ts[0:1, :])
         nc.gpsimd.memset(ts_window[0:LIVE_ROW, :], 0.0)
 
         bias_row = tile([P, P], F32, "bias_row")
-        nc.sync.dma_start(bias_row[LIVE_ROW:P, :], b.rearrange("(o n) -> o n", o=1))
+        nc.scalar.dma_start(bias_row[LIVE_ROW:P, :], b.rearrange("(o n) -> o n", o=1))
         nc.gpsimd.memset(bias_row[0:LIVE_ROW, :], 0.0)
 
         def load_words(a, window):
@@ -70,7 +70,10 @@ def tile_list_tabts_bias_kernel(tc, tab_words, tab_scales, w, ts, b, offs, out):
 
         def load_w(a, raw):
             nc.sync.dma_start(raw[:], w_rows[:, a, :])
-            nc.scalar.copy(w_bf16[a][:], raw[:].rearrange("p (i n) -> p n i", i=PACK))
+            nc.scalar.copy(
+                w_bf16[a][:].rearrange("p (c j) i -> p c i j", j=4),
+                raw[:].rearrange("p (i c j) -> p c i j", i=PACK, j=4),
+            )
 
         window0 = load_words(0, tile([P, T], I32, "word_window0"))
         load_w(0, tile([P, PACK * M], F32, "w_raw0"))
@@ -177,10 +180,17 @@ def tile_list_tabts_bias_kernel(tc, tab_words, tab_scales, w, ts, b, offs, out):
 
         scaled = tile([P, S], F32, "scaled")
         result = tile([P, S], F32, "result")
-        for r, (c0, c1) in enumerate(ranges):
-            nc.vector.tensor_tensor(scaled[:, c0:c1], sums[r][:], ts_spread[:, c0:c1], MULT)
-            if r < len(ranges) - 1:
-                nc.scalar.activation(result[:, c0:c1], scaled[:, c0:c1], IDENTITY, bias=bias[:])
-            else:
-                nc.vector.tensor_scalar_add(result[:, c0:c1], scaled[:, c0:c1], bias[:])
+        def scale(r, c0, c1):
+            first = ranges[r][0]
+            nc.vector.tensor_tensor(scaled[:, c0:c1], sums[r][:, c0 - first : c1 - first], ts_spread[:, c0:c1], MULT)
+
+        for c0 in range(0, 2 * N, N // 2):
+            c1 = c0 + N // 2
+            scale(c0 // N, c0, c1)
+            nc.scalar.activation(result[:, c0:c1], scaled[:, c0:c1], IDENTITY, bias=bias[:])
+            nc.sync.dma_start(out[:, c0:c1], result[:, c0:c1])
+        for r in (2, 3):
+            scale(r, *ranges[r])
+        for c0, c1 in ranges[2:]:
+            nc.vector.tensor_scalar_add(result[:, c0:c1], scaled[:, c0:c1], bias[:])
             nc.sync.dma_start(out[:, c0:c1], result[:, c0:c1])

@@ -86,12 +86,12 @@ def tile_list_tabts_bias_kernel(tc, tab_words, tab_scales, w, ts, b, offs, out):
         nc.vector.tensor_copy(scales_picked[:], scale_window[:].bitcast(U8).indirect(offsets[:]))
 
         def place_scales(i):
-            a, q = divmod(i, 4)
-            src = SCALE_BASE[a] + 4 * q
-            dst = 32 * q + 4 * a
+            a, r = divmod(i, 4)
+            src = SCALE_BASE[a] + r
+            dst = 4 * a + r
             nc.sync.dma_start(
-                planes[dst : dst + 4, a * (S // 4) : (a + 1) * (S // 4)],
-                scales_picked[src : src + 4, :].bitcast(I32),
+                planes[dst:P:32, a * (S // 4) : (a + 1) * (S // 4)],
+                scales_picked[src : src + 13 : 4, :].bitcast(I32),
             )
 
         for i in range(EARLY_MOVES):

@@ -50,8 +50,9 @@ def tile_list_tabts_bias_kernel(tc, tab_words, tab_scales, w, ts, b, offs, out):
             for c0, c1 in ((0, T // 4 - 1), (T // 4 - 1, T // 4)):
                 nc.vector.memset(scale_window[p0:p1, c0:c1], 0)
 
-        planes = tile([P, PASSES * S // 4], I32, "planes")
-        nc.gpsimd.memset(planes[:], 0)
+        planes = [tile([P, S // 4], I32, f"planes{a}") for a in range(PASSES)]
+        for plane in planes:
+            nc.gpsimd.memset(plane[:], 0)
 
         ts_window = tile([P, T], F32, "ts_window", "slot_ts_picked0")
         nc.scalar.dma_start(ts_window[LIVE_ROW:P, :], ts[0:1, :])
@@ -90,7 +91,7 @@ def tile_list_tabts_bias_kernel(tc, tab_words, tab_scales, w, ts, b, offs, out):
             src = SCALE_BASE[a] + r
             dst = 4 * a + r
             nc.sync.dma_start(
-                planes[dst:P:32, a * (S // 4) : (a + 1) * (S // 4)],
+                planes[a][dst:P:32, :],
                 scales_picked[src : src + 13 : 4, :].bitcast(I32),
             )
 
@@ -151,7 +152,7 @@ def tile_list_tabts_bias_kernel(tc, tab_words, tab_scales, w, ts, b, offs, out):
                 lhsT=w_codes[:, a * M : (a + 1) * M].bitcast(FP8X4),
                 lhsT_scale=w_scales[:, a * M : (a + 1) * M],
                 rhs=words[:, c0 - first : c1 - first].bitcast(FP8X4),
-                rhs_scale=planes[4 * a : P, (a * S + c0) // 4 : (a * S + c1) // 4].bitcast(U8),
+                rhs_scale=planes[a][4 * a : P, c0 // 4 : c1 // 4].bitcast(U8),
                 start=(a == 0),
                 stop=(a == PASSES - 1),
             )

@@ -24,8 +24,8 @@ N = 512
 SLICES = S // N
 BLOCKS = N // P
 LIVE_ROW = P - 1
-SCALE_BASE = (48, 96, 112)
-EARLY_MOVES = 6
+SCALE_BASE = (0, 16, 112)
+EARLY_MOVES = 4
 
 
 def tile_list_tabts_bias_kernel(tc, tab_words, tab_scales, w, ts, b, offs, out):
@@ -44,9 +44,9 @@ def tile_list_tabts_bias_kernel(tc, tab_words, tab_scales, w, ts, b, offs, out):
 
         scale_rows = tab_scales.rearrange("a q t -> (a q) t").bitcast(I32)
         scale_window = late.tile([P, T // 4], I32, name="scale_window", offset=4 * T - 1024)
-        nc.scalar.dma_start(scale_window[SCALE_BASE[0] : SCALE_BASE[0] + 16, :], scale_rows[0:16, :])
-        nc.sync.dma_start(scale_window[SCALE_BASE[1] : P, :], scale_rows[16:48, :])
-        for p0, p1 in ((0, SCALE_BASE[0]), (64, SCALE_BASE[1])):
+        nc.sync.dma_start(scale_window[0:32, :], scale_rows[0:32, :])
+        nc.scalar.dma_start(scale_window[SCALE_BASE[2] : P, :], scale_rows[32:48, :])
+        for p0, p1 in ((32, 64), (64, SCALE_BASE[2])):
             for c0, c1 in ((0, T // 4 - 1), (T // 4 - 1, T // 4)):
                 nc.vector.memset(scale_window[p0:p1, c0:c1], 0)
 
@@ -100,8 +100,8 @@ def tile_list_tabts_bias_kernel(tc, tab_words, tab_scales, w, ts, b, offs, out):
         window2 = load_words(2, late.tile([P, T], I32, name="word_window2", offset=0))
         for a in range(1, PASSES):
             load_w(a, late.tile([P, PACK * M], F32, name=f"w_raw{a}", offset=4 * T + (a - 1) * 4 * PACK * M))
-        for i in range(EARLY_MOVES, 4 * PASSES):
-            place_scales(i)
+            for i in range(4 * a, 4 * a + 4):
+                place_scales(i)
 
         ts_picked = tile([P, S], F32, "ts_picked")
         nc.vector.tensor_copy(ts_picked[:], ts_window[:].indirect(offsets[:]))

@@ -25,7 +25,6 @@ SLICES = S // N
 BLOCKS = N // P
 LIVE_ROW = P - 1
 SCALE_BASE = (0, 16, 112)
-EARLY_MOVES = 4
 
 
 def tile_list_tabts_bias_kernel(tc, tab_words, tab_scales, w, ts, b, offs, out):
@@ -95,13 +94,13 @@ def tile_list_tabts_bias_kernel(tc, tab_words, tab_scales, w, ts, b, offs, out):
                 scales_picked[src : src + 13 : 4, :].bitcast(I32),
             )
 
-        for i in range(EARLY_MOVES):
-            place_scales(i)
         window2 = load_words(2, late.tile([P, T], I32, name="word_window2", offset=0))
         for a in range(1, PASSES):
             load_w(a, late.tile([P, PACK * M], F32, name=f"w_raw{a}", offset=4 * T + (a - 1) * 4 * PACK * M))
-            for i in range(4 * a, 4 * a + 4):
+            for i in range(4 * a - 4, 4 * a):
                 place_scales(i)
+        for i in range(8, 12):
+            place_scales(i)
 
         ts_picked = tile([P, S], F32, "ts_picked")
         nc.vector.tensor_copy(ts_picked[:], ts_window[:].indirect(offsets[:]))

@@ -66,17 +66,20 @@ def tile_list_tabts_bias_kernel(tc, tab_words, tab_scales, w, ts, b, offs, out):
             return window
 
         w_rows = w.rearrange("(a p i) n -> p a (i n)", p=P, i=PACK)
-        w_bf16 = [tile([P, M, PACK], BF16, f"w_bf16_{a}", f"slot_w_last{a}") for a in range(PASSES)]
+        w_bf16_early = tile([P, 2, M * PACK], BF16, "w_bf16_early")
+        w_bf16_last = tile([P, M * PACK], BF16, "w_bf16_last", "slot_w_last2")
 
-        def load_w(a, raw):
-            nc.sync.dma_start(raw[:], w_rows[:, a, :])
+        def round_w(rounded, raw):
             nc.scalar.copy(
-                w_bf16[a][:].rearrange("p (c j) i -> p c i j", j=4),
-                raw[:].rearrange("p (i c j) -> p c i j", i=PACK, j=4),
+                rounded.rearrange("p (c j i) -> p c i j", j=4, i=PACK),
+                raw.rearrange("p (i c j) -> p c i j", i=PACK, j=4),
             )
 
         window0 = load_words(0, tile([P, T], I32, "word_window0"))
-        load_w(0, tile([P, PACK * M], F32, "w_raw0"))
+        w_raw_early = tile([P, 2, PACK * M], F32, "w_raw_early")
+        nc.sync.dma_start(w_raw_early[:], w_rows[:, 0:2, :])
+        for a in range(2):
+            round_w(w_bf16_early[:, a, :], w_raw_early[:, a, :])
         window1 = load_words(1, tile([P, T], I32, "word_window1"))
 
         identity = tile([P, P], F32, "identity")
@@ -95,11 +98,12 @@ def tile_list_tabts_bias_kernel(tc, tab_words, tab_scales, w, ts, b, offs, out):
             )
 
         window2 = load_words(2, late.tile([P, T], I32, name="word_window2", offset=0))
-        for a in range(1, PASSES):
-            load_w(a, late.tile([P, PACK * M], F32, name=f"w_raw{a}", offset=4 * T + (a - 1) * 4 * PACK * M))
-            for i in range(4 * a - 4, 4 * a):
-                place_scales(i)
-        for i in range(8, 12):
+        for i in range(4):
+            place_scales(i)
+        w_raw_last = late.tile([P, PACK * M], F32, name="w_raw_last", offset=4 * T)
+        nc.sync.dma_start(w_raw_last[:], w_rows[:, 2, :])
+        round_w(w_bf16_last[:], w_raw_last[:])
+        for i in range(4, 12):
             place_scales(i)
 
         ts_picked = tile([P, S], F32, "ts_picked")
@@ -137,11 +141,9 @@ def tile_list_tabts_bias_kernel(tc, tab_words, tab_scales, w, ts, b, offs, out):
         ranges = [(0, N), (N, 2 * N), (2 * N, 2 * N + N // 2), (2 * N + N // 2, S)]
         sums = [acc_pool.tile([P, c1 - c0], F32, name=f"sum{r}") for r, (c0, c1) in enumerate(ranges)]
 
-        def quantize_w(a):
+        def quantize_w(a0, a1, rounded):
             nc.vector.quantize_mx(
-                out=w_codes[:, a * M : (a + 1) * M].bitcast(FP8X4),
-                scales=w_scales[:, a * M : (a + 1) * M],
-                in_=w_bf16[a][:].rearrange("p n i -> p (n i)"),
+                out=w_codes[:, a0 * M : a1 * M].bitcast(FP8X4), scales=w_scales[:, a0 * M : a1 * M], in_=rounded
             )
 
         def multiply(a, r, words, first):
@@ -156,25 +158,21 @@ def tile_list_tabts_bias_kernel(tc, tab_words, tab_scales, w, ts, b, offs, out):
                 stop=(a == PASSES - 1),
             )
 
-        def gather_last(s):
-            words = tile([P, N], U32, f"picked_last{s}", f"slot_w_last{s}")
-            nc.vector.tensor_copy(
-                words[:], window2[:].bitcast(U32).indirect(offsets[:, s * (N // 16) : (s + 1) * (N // 16)])
-            )
+        def gather_last(c0, c1, slot=None):
+            words = tile([P, c1 - c0], U32, f"picked_last{c0}", slot)
+            nc.vector.tensor_copy(words[:], window2[:].bitcast(U32).indirect(offsets[:, c0 // 16 : c1 // 16]))
             return words
 
-        quantize_w(0)
+        quantize_w(0, 2, w_bf16_early[:].rearrange("p a c -> p (a c)"))
         for r in range(len(ranges)):
             multiply(0, r, picked[0], 0)
-        last0 = gather_last(0)
-        quantize_w(1)
         for r in range(len(ranges)):
             multiply(1, r, picked[1], 0)
-        last1 = gather_last(1)
-        quantize_w(2)
-        multiply(2, 0, last0, 0)
-        multiply(2, 1, last1, N)
-        last2 = gather_last(2)
+        head = gather_last(0, 2 * N)
+        quantize_w(2, 3, w_bf16_last[:])
+        multiply(2, 0, head, 0)
+        multiply(2, 1, head, 0)
+        last2 = gather_last(2 * N, S, "slot_w_last2")
         multiply(2, 2, last2, 2 * N)
         multiply(2, 3, last2, 2 * N)
 

@@ -45,17 +45,18 @@ def tile_list_tabts_bias_kernel(tc, tab_words, tab_scales, w, ts, b, offs, out):
         scale_window = late.tile([P, T // 4], I32, name="scale_window", offset=4 * T - 1024)
         nc.sync.dma_start(scale_window[0:32, :], scale_rows[0:32, :])
         nc.scalar.dma_start(scale_window[SCALE_BASE[2] : P, :], scale_rows[32:48, :])
-        for p0, p1 in ((32, 64), (64, SCALE_BASE[2])):
-            for c0, c1 in ((0, T // 4 - 1), (T // 4 - 1, T // 4)):
-                nc.vector.memset(scale_window[p0:p1, c0:c1], 0)
+        for c0, c1 in ((0, T // 4 - 1), (T // 4 - 1, T // 4)):
+            nc.vector.memset(scale_window[32:64, c0:c1], 0)
+        nc.gpsimd.memset(scale_window[64 : SCALE_BASE[2], :], 0)
 
         planes = [tile([P, S // 4], I32, f"planes{a}") for a in range(PASSES)]
-        for plane in planes:
-            nc.gpsimd.memset(plane[:], 0)
+        nc.gpsimd.memset(planes[0][:], 0)
 
         ts_window = tile([P, T], F32, "ts_window", "slot_ts_picked0")
         nc.scalar.dma_start(ts_window[LIVE_ROW:P, :], ts[0:1, :])
-        nc.gpsimd.memset(ts_window[0:LIVE_ROW, :], 0.0)
+        for c0, c1 in ((0, N - 1), (N - 1, N)):
+            nc.vector.memset(ts_window[0:LIVE_ROW, c0:c1], 0.0)
+        nc.gpsimd.memset(ts_window[0:LIVE_ROW, N:T], 0.0)
 
         bias_row = tile([P, P], F32, "bias_row")
         nc.scalar.dma_start(bias_row[LIVE_ROW:P, :], b.rearrange("(o n) -> o n", o=1))
@@ -84,6 +85,8 @@ def tile_list_tabts_bias_kernel(tc, tab_words, tab_scales, w, ts, b, offs, out):
 
         identity = tile([P, P], F32, "identity")
         make_identity(nc, identity[:])
+        for plane in planes[1:]:
+            nc.gpsimd.memset(plane[:], 0)
 
         scales_picked = tile([P, S], U8, "scales_picked")
         nc.vector.tensor_copy(scales_picked[:], scale_window[:].bitcast(U8).indirect(offsets[:]))
@@ -182,8 +185,8 @@ def tile_list_tabts_bias_kernel(tc, tab_words, tab_scales, w, ts, b, offs, out):
             first = ranges[r][0]
             nc.vector.tensor_tensor(scaled[:, c0:c1], sums[r][:, c0 - first : c1 - first], ts_spread[:, c0:c1], MULT)
 
-        for c0 in range(0, 2 * N, N // 2):
-            c1 = c0 + N // 2
+        cuts = (0, P, 2 * P, N, N + N // 2, 2 * N)
+        for c0, c1 in zip(cuts, cuts[1:]):
             scale(c0 // N, c0, c1)
             nc.scalar.activation(result[:, c0:c1], scaled[:, c0:c1], IDENTITY, bias=bias[:])
             nc.sync.dma_start(out[:, c0:c1], result[:, c0:c1])

@@ -18,13 +18,17 @@ MULT = mybir.AluOpType.mult
 IDENTITY = mybir.ActivationFunctionType.Identity
 
 P = 128
+QUADRANT = 32
 PACK = 4
 PASSES = K // (P * PACK)
+SCALE_ROWS = 16
 N = 512
+HALF = N // 2
 SLICES = S // N
 BLOCKS = N // P
 LIVE_ROW = P - 1
-SCALE_BASE = (0, 16, 112)
+SCALE_BASE = (0, SCALE_ROWS, P - SCALE_ROWS)
+TS_ZEROED_BY_VECTOR = 384
 
 
 def tile_list_tabts_bias_kernel(tc, tab_words, tab_scales, w, ts, b, offs, out):
@@ -38,25 +42,28 @@ def tile_list_tabts_bias_kernel(tc, tab_words, tab_scales, w, ts, b, offs, out):
         def tile(shape, dtype, name, slot=None):
             return keep.tile(shape, dtype, name=name, tag=slot or name, align_bytes=64)
 
+        def zero_on_vector(rows, columns):
+            for c0, c1 in ((0, columns - 1), (columns - 1, columns)):
+                nc.vector.memset(rows[:, c0:c1], 0)
+
         offsets = keep.tile([P, S // 16], U16, name="offsets")
         nc.sync.dma_start(offsets[:], offs)
 
+        word_window_bytes = 4 * T
         scale_rows = tab_scales.rearrange("a q t -> (a q) t").bitcast(I32)
-        scale_window = late.tile([P, T // 4], I32, name="scale_window", offset=4 * T - 1024)
-        nc.sync.dma_start(scale_window[0:32, :], scale_rows[0:32, :])
-        nc.scalar.dma_start(scale_window[SCALE_BASE[2] : P, :], scale_rows[32:48, :])
-        for c0, c1 in ((0, T // 4 - 1), (T // 4 - 1, T // 4)):
-            nc.vector.memset(scale_window[32:64, c0:c1], 0)
-        nc.gpsimd.memset(scale_window[64 : SCALE_BASE[2], :], 0)
+        scale_window = late.tile([P, T // 4], I32, name="scale_window", offset=word_window_bytes - T // 4)
+        nc.sync.dma_start(scale_window[0:QUADRANT, :], scale_rows[0 : 2 * SCALE_ROWS, :])
+        nc.scalar.dma_start(scale_window[SCALE_BASE[2] : P, :], scale_rows[2 * SCALE_ROWS : 3 * SCALE_ROWS, :])
+        zero_on_vector(scale_window[QUADRANT : 2 * QUADRANT, :], T // 4)
+        nc.gpsimd.memset(scale_window[2 * QUADRANT : SCALE_BASE[2], :], 0)
 
         planes = [tile([P, S // 4], I32, f"planes{a}") for a in range(PASSES)]
         nc.gpsimd.memset(planes[0][:], 0)
 
         ts_window = tile([P, T], F32, "ts_window", "slot_ts_picked0")
-        nc.scalar.dma_start(ts_window[LIVE_ROW:P, :], ts[0:1, :])
-        for c0, c1 in ((0, N - 1), (N - 1, N)):
-            nc.vector.memset(ts_window[0:LIVE_ROW, c0:c1], 0.0)
-        nc.gpsimd.memset(ts_window[0:LIVE_ROW, N:T], 0.0)
+        nc.sync.dma_start(ts_window[LIVE_ROW:P, :], ts[0:1, :])
+        zero_on_vector(ts_window[0:LIVE_ROW, :], TS_ZEROED_BY_VECTOR)
+        nc.gpsimd.memset(ts_window[0:LIVE_ROW, TS_ZEROED_BY_VECTOR:T], 0.0)
 
         bias_row = tile([P, P], F32, "bias_row")
         nc.scalar.dma_start(bias_row[LIVE_ROW:P, :], b.rearrange("(o n) -> o n", o=1))
@@ -91,23 +98,21 @@ def tile_list_tabts_bias_kernel(tc, tab_words, tab_scales, w, ts, b, offs, out):
         scales_picked = tile([P, S], U8, "scales_picked")
         nc.vector.tensor_copy(scales_picked[:], scale_window[:].bitcast(U8).indirect(offsets[:]))
 
-        def place_scales(i):
-            a, r = divmod(i, 4)
-            src = SCALE_BASE[a] + r
-            dst = 4 * a + r
-            nc.sync.dma_start(
-                planes[a][dst:P:32, :],
-                scales_picked[src : src + 13 : 4, :].bitcast(I32),
-            )
+        def place_scales(a):
+            for r in range(4):
+                first = SCALE_BASE[a] + r
+                nc.sync.dma_start(
+                    planes[a][4 * a + r : P : QUADRANT, :],
+                    scales_picked[first : first + 3 * 4 + 1 : 4, :].bitcast(I32),
+                )
 
         window2 = load_words(2, late.tile([P, T], I32, name="word_window2", offset=0))
-        for i in range(4):
-            place_scales(i)
-        w_raw_last = late.tile([P, PACK * M], F32, name="w_raw_last", offset=4 * T)
+        place_scales(0)
+        w_raw_last = late.tile([P, PACK * M], F32, name="w_raw_last", offset=word_window_bytes)
         nc.sync.dma_start(w_raw_last[:], w_rows[:, 2, :])
         round_w(w_bf16_last[:], w_raw_last[:])
-        for i in range(4, 12):
-            place_scales(i)
+        for a in range(1, PASSES):
+            place_scales(a)
 
         ts_picked = tile([P, S], F32, "ts_picked")
         nc.vector.tensor_copy(ts_picked[:], ts_window[:].indirect(offsets[:]))
@@ -129,9 +134,11 @@ def tile_list_tabts_bias_kernel(tc, tab_words, tab_scales, w, ts, b, offs, out):
         for s in range(SLICES):
             spread = flip_pool.tile([P, N], F32, name="spread")
             for i in range(BLOCKS):
-                c = s * BLOCKS + i
+                column = s * BLOCKS + i
                 nc.tensor.transpose(
-                    spread[:, i * P : (i + 1) * P], ts_columns[:, c : c + 1].to_broadcast([P, P]), identity[:]
+                    spread[:, i * P : (i + 1) * P],
+                    ts_columns[:, column : column + 1].to_broadcast([P, P]),
+                    identity[:],
                 )
             nc.scalar.copy(ts_spread[:, s * N : (s + 1) * N], spread[:])
 
@@ -141,57 +148,59 @@ def tile_list_tabts_bias_kernel(tc, tab_words, tab_scales, w, ts, b, offs, out):
 
         w_codes = tile([P, PASSES * M], U32, "w_codes")
         w_scales = tile([P, PASSES * M], U8, "w_scales")
-        ranges = [(0, N), (N, 2 * N), (2 * N, 2 * N + N // 2), (2 * N + N // 2, S)]
-        sums = [acc_pool.tile([P, c1 - c0], F32, name=f"sum{r}") for r, (c0, c1) in enumerate(ranges)]
+        ranges = [(0, N), (N, 2 * N), (2 * N, 2 * N + HALF), (2 * N + HALF, S)]
+        sums = [acc_pool.tile([P, c1 - c0], F32, name=f"sum{g}") for g, (c0, c1) in enumerate(ranges)]
 
         def quantize_w(a0, a1, rounded):
             nc.vector.quantize_mx(
                 out=w_codes[:, a0 * M : a1 * M].bitcast(FP8X4), scales=w_scales[:, a0 * M : a1 * M], in_=rounded
             )
 
-        def multiply(a, r, words, first):
-            c0, c1 = ranges[r]
+        def multiply(a, g, words, words_from):
+            c0, c1 = ranges[g]
             nc.tensor.matmul_mx(
-                out=sums[r][:],
+                out=sums[g][:],
                 lhsT=w_codes[:, a * M : (a + 1) * M].bitcast(FP8X4),
                 lhsT_scale=w_scales[:, a * M : (a + 1) * M],
-                rhs=words[:, c0 - first : c1 - first].bitcast(FP8X4),
+                rhs=words[:, c0 - words_from : c1 - words_from].bitcast(FP8X4),
                 rhs_scale=planes[a][4 * a : P, c0 // 4 : c1 // 4].bitcast(U8),
                 start=(a == 0),
                 stop=(a == PASSES - 1),
             )
 
-        def gather_last(c0, c1, slot=None):
+        def gather_pass2(c0, c1, slot=None):
             words = tile([P, c1 - c0], U32, f"picked_last{c0}", slot)
             nc.vector.tensor_copy(words[:], window2[:].bitcast(U32).indirect(offsets[:, c0 // 16 : c1 // 16]))
             return words
 
         quantize_w(0, 2, w_bf16_early[:].rearrange("p a c -> p (a c)"))
-        for r in range(len(ranges)):
-            multiply(0, r, picked[0], 0)
-        for r in range(len(ranges)):
-            multiply(1, r, picked[1], 0)
-        head = gather_last(0, 2 * N)
+        for a in range(2):
+            for g in range(len(ranges)):
+                multiply(a, g, picked[a], 0)
+        head = gather_pass2(0, 2 * N)
         quantize_w(2, 3, w_bf16_last[:])
-        multiply(2, 0, head, 0)
-        multiply(2, 1, head, 0)
-        last2 = gather_last(2 * N, S, "slot_w_last2")
-        multiply(2, 2, last2, 2 * N)
-        multiply(2, 3, last2, 2 * N)
+        for g in (0, 1):
+            multiply(2, g, head, 0)
+        tail = gather_pass2(2 * N, S, "slot_w_last2")
+        for g in (2, 3):
+            multiply(2, g, tail, 2 * N)
 
         scaled = tile([P, S], F32, "scaled")
         result = tile([P, S], F32, "result")
-        def scale(r, c0, c1):
-            first = ranges[r][0]
-            nc.vector.tensor_tensor(scaled[:, c0:c1], sums[r][:, c0 - first : c1 - first], ts_spread[:, c0:c1], MULT)
 
-        cuts = (0, P, 2 * P, N, N + N // 2, 2 * N)
+        def scale(g, c0, c1):
+            sum_from = ranges[g][0]
+            nc.vector.tensor_tensor(
+                scaled[:, c0:c1], sums[g][:, c0 - sum_from : c1 - sum_from], ts_spread[:, c0:c1], MULT
+            )
+
+        cuts = (0, P, HALF, N, N + HALF, 2 * N)
         for c0, c1 in zip(cuts, cuts[1:]):
             scale(c0 // N, c0, c1)
             nc.scalar.activation(result[:, c0:c1], scaled[:, c0:c1], IDENTITY, bias=bias[:])
             nc.sync.dma_start(out[:, c0:c1], result[:, c0:c1])
-        for r in (2, 3):
-            scale(r, *ranges[r])
+        for g in (2, 3):
+            scale(g, *ranges[g])
         for c0, c1 in ranges[2:]:
             nc.vector.tensor_scalar_add(result[:, c0:c1], scaled[:, c0:c1], bias[:])
             nc.sync.dma_start(out[:, c0:c1], result[:, c0:c1])

@@ -60,7 +60,7 @@ def tile_list_tabts_bias_kernel(tc, tab_words, tab_scales, w, ts, b, offs, out):
         planes = [tile([P, S // 4], I32, f"planes{a}") for a in range(PASSES)]
         nc.gpsimd.memset(planes[0][:], 0)
 
-        ts_window = tile([P, T], F32, "ts_window", "slot_ts_picked0")
+        ts_window = tile([P, T], F32, "ts_window")
         nc.sync.dma_start(ts_window[LIVE_ROW:P, :], ts[0:1, :])
         zero_on_vector(ts_window[0:LIVE_ROW, :], TS_ZEROED_BY_VECTOR)
         nc.gpsimd.memset(ts_window[0:LIVE_ROW, TS_ZEROED_BY_VECTOR:T], 0.0)
@@ -75,7 +75,7 @@ def tile_list_tabts_bias_kernel(tc, tab_words, tab_scales, w, ts, b, offs, out):
 
         w_rows = w.rearrange("(a p i) n -> p a (i n)", p=P, i=PACK)
         w_bf16_early = tile([P, 2, M * PACK], BF16, "w_bf16_early")
-        w_bf16_last = tile([P, M * PACK], BF16, "w_bf16_last", "slot_w_last2")
+        w_bf16_last = tile([P, M * PACK], BF16, "w_bf16_last")
 
         def round_w(rounded, raw):
             nc.scalar.copy(
@@ -142,7 +142,7 @@ def tile_list_tabts_bias_kernel(tc, tab_words, tab_scales, w, ts, b, offs, out):
                 )
             nc.scalar.copy(ts_spread[:, s * N : (s + 1) * N], spread[:])
 
-        picked = [tile([P, S], U32, "picked0", "slot_ts_picked0"), tile([P, S], U32, "picked1")]
+        picked = [tile([P, S], U32, "picked0"), tile([P, S], U32, "picked1")]
         nc.vector.tensor_copy(picked[0][:], window0[:].bitcast(U32).indirect(offsets[:]))
         nc.vector.tensor_copy(picked[1][:], window1[:].bitcast(U32).indirect(offsets[:]))
 
@@ -168,8 +168,7 @@ def tile_list_tabts_bias_kernel(tc, tab_words, tab_scales, w, ts, b, offs, out):
                 stop=(a == PASSES - 1),
             )
 
-        def gather_pass2(c0, c1, slot=None):
-            words = tile([P, c1 - c0], U32, f"picked_last{c0}", slot)
+        def gather_pass2(c0, c1, words):
             nc.vector.tensor_copy(words[:], window2[:].bitcast(U32).indirect(offsets[:, c0 // 16 : c1 // 16]))
             return words
 
@@ -177,11 +176,13 @@ def tile_list_tabts_bias_kernel(tc, tab_words, tab_scales, w, ts, b, offs, out):
         for a in range(2):
             for g in range(len(ranges)):
                 multiply(a, g, picked[a], 0)
-        head = gather_pass2(0, 2 * N)
+        head = gather_pass2(0, 2 * N, tile([P, 2 * N], U32, "picked_head"))
         quantize_w(2, 3, w_bf16_last[:])
         for g in (0, 1):
             multiply(2, g, head, 0)
-        tail = gather_pass2(2 * N, S, "slot_w_last2")
+        tail = gather_pass2(
+            2 * N, S, late.tile([P, N], U32, name="picked_tail", offset=word_window_bytes, align_bytes=64)
+        )
         for g in (2, 3):
             multiply(2, g, tail, 2 * N)
 

@@ -28,7 +28,7 @@ SLICES = S // N
 BLOCKS = N // P
 LIVE_ROW = P - 1
 SCALE_BASE = (0, SCALE_ROWS, P - SCALE_ROWS)
-TS_ZEROED_BY_VECTOR = 384
+TS_ZEROED_BY_VECTOR = 128
 
 
 def tile_list_tabts_bias_kernel(tc, tab_words, tab_scales, w, ts, b, offs, out):
@@ -58,7 +58,10 @@ def tile_list_tabts_bias_kernel(tc, tab_words, tab_scales, w, ts, b, offs, out):
         nc.gpsimd.memset(scale_window[2 * QUADRANT : SCALE_BASE[2], :], 0)
 
         planes = [tile([P, S // 4], I32, f"planes{a}") for a in range(PASSES)]
-        nc.gpsimd.memset(planes[0][:], 0)
+
+        w_rows = w.rearrange("(a p i) n -> p a (i n)", p=P, i=PACK)
+        w_raw_early = tile([P, 2, PACK * M], F32, "w_raw_early")
+        nc.sync.dma_start(w_raw_early[:], w_rows[:, 0:2, :])
 
         ts_window = tile([P, T], F32, "ts_window")
         nc.sync.dma_start(ts_window[LIVE_ROW:P, :], ts[0:1, :])
@@ -73,7 +76,6 @@ def tile_list_tabts_bias_kernel(tc, tab_words, tab_scales, w, ts, b, offs, out):
             nc.sync.dma_start(window[:], tab_words[a].rearrange("p t i -> p (t i)").bitcast(I32))
             return window
 
-        w_rows = w.rearrange("(a p i) n -> p a (i n)", p=P, i=PACK)
         w_bf16_early = tile([P, 2, M * PACK], BF16, "w_bf16_early")
         w_bf16_last = tile([P, M * PACK], BF16, "w_bf16_last")
 
@@ -84,15 +86,13 @@ def tile_list_tabts_bias_kernel(tc, tab_words, tab_scales, w, ts, b, offs, out):
             )
 
         window0 = load_words(0, tile([P, T], I32, "word_window0"))
-        w_raw_early = tile([P, 2, PACK * M], F32, "w_raw_early")
-        nc.sync.dma_start(w_raw_early[:], w_rows[:, 0:2, :])
         for a in range(2):
             round_w(w_bf16_early[:, a, :], w_raw_early[:, a, :])
         window1 = load_words(1, tile([P, T], I32, "word_window1"))
 
         identity = tile([P, P], F32, "identity")
         make_identity(nc, identity[:])
-        for plane in planes[1:]:
+        for plane in planes:
             nc.gpsimd.memset(plane[:], 0)
 
         scales_picked = tile([P, S], U8, "scales_picked")

@@ -98,8 +98,8 @@ def tile_list_tabts_bias_kernel(tc, tab_words, tab_scales, w, ts, b, offs, out):
         scales_picked = tile([P, S], U8, "scales_picked")
         nc.vector.tensor_copy(scales_picked[:], scale_window[:].bitcast(U8).indirect(offsets[:]))
 
-        def place_scales(a):
-            for r in range(4):
+        def place_scales(a, rows=range(4)):
+            for r in rows:
                 first = SCALE_BASE[a] + r
                 nc.sync.dma_start(
                     planes[a][4 * a + r : P : QUADRANT, :],
@@ -107,12 +107,13 @@ def tile_list_tabts_bias_kernel(tc, tab_words, tab_scales, w, ts, b, offs, out):
                 )
 
         window2 = load_words(2, late.tile([P, T], I32, name="word_window2", offset=0))
-        place_scales(0)
+        place_scales(0, range(0, 4))
+        place_scales(1, range(2))
         w_raw_last = late.tile([P, PACK * M], F32, name="w_raw_last", offset=word_window_bytes)
         nc.sync.dma_start(w_raw_last[:], w_rows[:, 2, :])
         round_w(w_bf16_last[:], w_raw_last[:])
-        for a in range(1, PASSES):
-            place_scales(a)
+        place_scales(1, range(2, 4))
+        place_scales(2)
 
         ts_picked = tile([P, S], F32, "ts_picked")
         nc.vector.tensor_copy(ts_picked[:], ts_window[:].indirect(offsets[:]))
@@ -149,6 +150,7 @@ def tile_list_tabts_bias_kernel(tc, tab_words, tab_scales, w, ts, b, offs, out):
         w_codes = tile([P, PASSES * M], U32, "w_codes")
         w_scales = tile([P, PASSES * M], U8, "w_scales")
         ranges = [(0, N), (N, 2 * N), (2 * N, 2 * N + HALF), (2 * N + HALF, S)]
+        last_pass = [2, 1, 1, 1]
         sums = [acc_pool.tile([P, c1 - c0], F32, name=f"sum{g}") for g, (c0, c1) in enumerate(ranges)]
 
         def quantize_w(a0, a1, rounded):
@@ -165,7 +167,7 @@ def tile_list_tabts_bias_kernel(tc, tab_words, tab_scales, w, ts, b, offs, out):
                 rhs=words[:, c0 - words_from : c1 - words_from].bitcast(FP8X4),
                 rhs_scale=planes[a][4 * a : P, c0 // 4 : c1 // 4].bitcast(U8),
                 start=(a == 0),
-                stop=(a == PASSES - 1),
+                stop=(a == last_pass[g]),
             )
 
         def gather_pass2(c0, c1, words):
@@ -173,18 +175,20 @@ def tile_list_tabts_bias_kernel(tc, tab_words, tab_scales, w, ts, b, offs, out):
             return words
 
         quantize_w(0, 2, w_bf16_early[:].rearrange("p a c -> p (a c)"))
-        for a in range(2):
-            for g in range(len(ranges)):
-                multiply(a, g, picked[a], 0)
+        for g in range(len(ranges)):
+            multiply(0, g, picked[0], 0)
+        multiply(1, 0, picked[1], 0)
         head = gather_pass2(0, 2 * N, tile([P, 2 * N], U32, "picked_head"))
         quantize_w(2, 3, w_bf16_last[:])
         for g in (0, 1):
             multiply(2, g, head, 0)
+        multiply(1, 1, picked[1], 0)
         tail = gather_pass2(
             2 * N, S, late.tile([P, N], U32, name="picked_tail", offset=word_window_bytes, align_bytes=64)
         )
         for g in (2, 3):
             multiply(2, g, tail, 2 * N)
+            multiply(1, g, picked[1], 0)
 
         scaled = tile([P, S], F32, "scaled")
         result = tile([P, S], F32, "result")

@@ -27,7 +27,8 @@ HALF = N // 2
 SLICES = S // N
 BLOCKS = N // P
 LIVE_ROW = P - 1
-SCALE_BASE = (0, SCALE_ROWS, P - SCALE_ROWS)
+SCALE_FIRST = 3 * QUADRANT - PASSES * SCALE_ROWS
+SCALE_END = 3 * QUADRANT
 TS_ZEROED_BY_VECTOR = 128
 
 
@@ -52,10 +53,13 @@ def tile_list_tabts_bias_kernel(tc, tab_words, tab_scales, w, ts, b, offs, out):
         word_window_bytes = 4 * T
         scale_rows = tab_scales.rearrange("a q t -> (a q) t").bitcast(I32)
         scale_window = late.tile([P, T // 4], I32, name="scale_window", offset=word_window_bytes - T // 4)
-        nc.sync.dma_start(scale_window[0:QUADRANT, :], scale_rows[0 : 2 * SCALE_ROWS, :])
-        nc.scalar.dma_start(scale_window[SCALE_BASE[2] : P, :], scale_rows[2 * SCALE_ROWS : 3 * SCALE_ROWS, :])
-        zero_on_vector(scale_window[QUADRANT : 2 * QUADRANT, :], T // 4)
-        nc.gpsimd.memset(scale_window[2 * QUADRANT : SCALE_BASE[2], :], 0)
+        for a in range(PASSES):
+            nc.sync.dma_start(
+                scale_window[SCALE_FIRST + a : SCALE_END : PASSES, :],
+                scale_rows[a * SCALE_ROWS : (a + 1) * SCALE_ROWS, :],
+            )
+        zero_on_vector(scale_window[0:SCALE_FIRST, :], T // 4)
+        nc.gpsimd.memset(scale_window[SCALE_END:P, :], 0)
 
         planes = [tile([P, S // 4], I32, f"planes{a}") for a in range(PASSES)]
 
@@ -100,10 +104,10 @@ def tile_list_tabts_bias_kernel(tc, tab_words, tab_scales, w, ts, b, offs, out):
 
         def place_scales(a, rows=range(4)):
             for r in rows:
-                first = SCALE_BASE[a] + r
+                first = SCALE_FIRST + PASSES * r + a
                 nc.sync.dma_start(
                     planes[a][4 * a + r : P : QUADRANT, :],
-                    scales_picked[first : first + 3 * 4 + 1 : 4, :].bitcast(I32),
+                    scales_picked[first:SCALE_END : 4 * PASSES, :].bitcast(I32),
                 )
 
         window2 = load_words(2, late.tile([P, T], I32, name="word_window2", offset=0))

@@ -29,7 +29,7 @@ BLOCKS = N // P
 LIVE_ROW = P - 1
 SCALE_FIRST = 3 * QUADRANT - PASSES * SCALE_ROWS
 SCALE_END = 3 * QUADRANT
-TS_ZEROED_BY_VECTOR = 128
+TS_ZEROED_BY_VECTOR = 384
 
 
 def tile_list_tabts_bias_kernel(tc, tab_words, tab_scales, w, ts, b, offs, out):

@@ -29,7 +29,8 @@ BLOCKS = N // P
 LIVE_ROW = P - 1
 SCALE_FIRST = 3 * QUADRANT - PASSES * SCALE_ROWS
 SCALE_END = 3 * QUADRANT
-TS_ZEROED_BY_VECTOR = 384
+TS_ZEROED_BY_VECTOR = 768
+TURNED = 512
 
 
 def tile_list_tabts_bias_kernel(tc, tab_words, tab_scales, w, ts, b, offs, out):
@@ -50,9 +51,14 @@ def tile_list_tabts_bias_kernel(tc, tab_words, tab_scales, w, ts, b, offs, out):
         offsets = keep.tile([P, S // 16], U16, name="offsets")
         nc.sync.dma_start(offsets[:], offs)
 
-        word_window_bytes = 4 * T
+        def late_tile(shape, dtype, name, offset):
+            return late.tile(shape, dtype, name=name, offset=offset, align_bytes=64)
+
+        window_bytes = 4 * T
+        w_last_at = window_bytes + 4 * N
+        w_last_end = w_last_at + 4 * PACK * M
         scale_rows = tab_scales.rearrange("a q t -> (a q) t").bitcast(I32)
-        scale_window = late.tile([P, T // 4], I32, name="scale_window", offset=word_window_bytes - T // 4)
+        scale_window = late_tile([P, T // 4], I32, "scale_window", window_bytes - 64)
         for a in range(PASSES):
             nc.sync.dma_start(
                 scale_window[SCALE_FIRST + a : SCALE_END : PASSES, :],
@@ -61,7 +67,10 @@ def tile_list_tabts_bias_kernel(tc, tab_words, tab_scales, w, ts, b, offs, out):
         zero_on_vector(scale_window[0:SCALE_FIRST, :], T // 4)
         nc.gpsimd.memset(scale_window[SCALE_END:P, :], 0)
 
-        planes = [tile([P, S // 4], I32, f"planes{a}") for a in range(PASSES)]
+        planes = [tile([P, S // 4], I32, f"planes{a}") for a in range(2)]
+        planes.append(tile([P, 2 * N // 4], I32, "planes2"))
+        for plane in planes[:2]:
+            nc.gpsimd.memset(plane[:], 0)
 
         w_rows = w.rearrange("(a p i) n -> p a (i n)", p=P, i=PACK)
         w_raw_early = tile([P, 2, PACK * M], F32, "w_raw_early")
@@ -96,56 +105,60 @@ def tile_list_tabts_bias_kernel(tc, tab_words, tab_scales, w, ts, b, offs, out):
 
         identity = tile([P, P], F32, "identity")
         make_identity(nc, identity[:])
-        for plane in planes:
-            nc.gpsimd.memset(plane[:], 0)
+        nc.gpsimd.memset(planes[2][:], 0)
 
         scales_picked = tile([P, S], U8, "scales_picked")
         nc.vector.tensor_copy(scales_picked[:], scale_window[:].bitcast(U8).indirect(offsets[:]))
 
-        def place_scales(a, rows=range(4)):
-            for r in rows:
+        def place_scales(a, plane, c0, c1):
+            for r in range(4):
                 first = SCALE_FIRST + PASSES * r + a
                 nc.sync.dma_start(
-                    planes[a][4 * a + r : P : QUADRANT, :],
-                    scales_picked[first:SCALE_END : 4 * PASSES, :].bitcast(I32),
+                    plane[4 * a + r : P : QUADRANT, :],
+                    scales_picked[first:SCALE_END : 4 * PASSES, c0:c1].bitcast(I32),
                 )
 
-        window2 = load_words(2, late.tile([P, T], I32, name="word_window2", offset=0))
-        place_scales(0, range(0, 4))
-        place_scales(1, range(2))
-        w_raw_last = late.tile([P, PACK * M], F32, name="w_raw_last", offset=word_window_bytes)
+        place_scales(0, planes[0], 0, S)
+        window2 = late_tile([P, T], I32, "word_window2", 0)
+        words2 = tab_words[2].rearrange("p t i -> p (t i)").bitcast(I32)
+        nc.sync.dma_start(window2[:, 0 : T // 2], words2[:, 0 : T // 2])
+        place_scales(1, planes[1], 0, S)
+        nc.sync.dma_start(window2[:, T // 2 : T], words2[:, T // 2 : T])
+        w_raw_last = late_tile([P, PACK * M], F32, "w_raw_last", w_last_at)
         nc.sync.dma_start(w_raw_last[:], w_rows[:, 2, :])
+        place_scales(2, planes[2], 0, 2 * N)
         round_w(w_bf16_last[:], w_raw_last[:])
-        place_scales(1, range(2, 4))
-        place_scales(2)
+        plane_last = tile([P, N // 4], I32, "plane_last")
+        nc.gpsimd.memset(plane_last[:], 0)
+        place_scales(2, plane_last, 2 * N, S)
 
         ts_picked = tile([P, S], F32, "ts_picked")
         nc.vector.tensor_copy(ts_picked[:], ts_window[:].indirect(offsets[:]))
 
         ts_columns = tile([P, SLICES * BLOCKS], F32, "ts_columns")
-        ts_spread = tile([P, S], F32, "ts_spread")
+        ts_spread = tile([P, S - TURNED], F32, "ts_spread")
         for s in range(SLICES):
-            turned = flip_pool.tile([P, BLOCKS, P], F32, name="turned")
+            turned = flip_pool.tile([P, BLOCKS, P], F32, name="turned", tag="flip")
             for i in range(BLOCKS):
                 c0 = s * N + i * P
                 nc.tensor.transpose(turned[:, i, :], ts_picked[:, c0 : c0 + P], identity[:])
             nc.scalar.copy(ts_columns[:, s * BLOCKS : (s + 1) * BLOCKS], turned[:, :, LIVE_ROW])
 
         bias = tile([P, 1], F32, "bias")
-        turned = flip_pool.tile([P, BLOCKS, P], F32, name="turned")
+        turned = flip_pool.tile([P, BLOCKS, P], F32, name="turned", tag="flip")
         nc.tensor.transpose(turned[:, 0, :], bias_row[:], identity[:])
         nc.scalar.copy(bias[:], turned[:, 0, LIVE_ROW:P])
 
-        for s in range(SLICES):
-            spread = flip_pool.tile([P, N], F32, name="spread")
-            for i in range(BLOCKS):
-                column = s * BLOCKS + i
+        for c0 in range(TURNED, S, HALF):
+            spread = flip_pool.tile([P, HALF], F32, name="spread", tag="flip")
+            for i in range(HALF // P):
+                column = c0 // P + i
                 nc.tensor.transpose(
                     spread[:, i * P : (i + 1) * P],
                     ts_columns[:, column : column + 1].to_broadcast([P, P]),
                     identity[:],
                 )
-            nc.scalar.copy(ts_spread[:, s * N : (s + 1) * N], spread[:])
+            nc.scalar.copy(ts_spread[:, c0 - TURNED : c0 - TURNED + HALF], spread[:])
 
         picked = [tile([P, S], U32, "picked0"), tile([P, S], U32, "picked1")]
         nc.vector.tensor_copy(picked[0][:], window0[:].bitcast(U32).indirect(offsets[:]))
@@ -153,63 +166,114 @@ def tile_list_tabts_bias_kernel(tc, tab_words, tab_scales, w, ts, b, offs, out):
 
         w_codes = tile([P, PASSES * M], U32, "w_codes")
         w_scales = tile([P, PASSES * M], U8, "w_scales")
-        ranges = [(0, N), (N, 2 * N), (2 * N, 2 * N + HALF), (2 * N + HALF, S)]
-        last_pass = [2, 1, 1, 1]
-        sums = [acc_pool.tile([P, c1 - c0], F32, name=f"sum{g}") for g, (c0, c1) in enumerate(ranges)]
+        starts = range(0, S, HALF)
+        sums = [acc_pool.tile([P, HALF], F32, name=f"sum{g}") for g in range(len(starts))]
 
         def quantize_w(a0, a1, rounded):
             nc.vector.quantize_mx(
                 out=w_codes[:, a0 * M : a1 * M].bitcast(FP8X4), scales=w_scales[:, a0 * M : a1 * M], in_=rounded
             )
 
-        def multiply(a, g, words, words_from):
-            c0, c1 = ranges[g]
-            nc.tensor.matmul_mx(
-                out=sums[g][:],
-                lhsT=w_codes[:, a * M : (a + 1) * M].bitcast(FP8X4),
-                lhsT_scale=w_scales[:, a * M : (a + 1) * M],
-                rhs=words[:, c0 - words_from : c1 - words_from].bitcast(FP8X4),
-                rhs_scale=planes[a][4 * a : P, c0 // 4 : c1 // 4].bitcast(U8),
-                start=(a == 0),
-                stop=(a == last_pass[g]),
-            )
+        def multiply(a, g, words, words_from, plane, plane_from):
+            c0 = starts[g]
+            codes, scales = w_codes[:, a * M : (a + 1) * M].bitcast(FP8X4), w_scales[:, a * M : (a + 1) * M]
 
-        def gather_pass2(c0, c1, words):
-            nc.vector.tensor_copy(words[:], window2[:].bitcast(U32).indirect(offsets[:, c0 // 16 : c1 // 16]))
+            def table(t0, t1):
+                return (
+                    words[:, t0 - words_from : t1 - words_from].bitcast(FP8X4),
+                    plane[4 * a : P, (t0 - plane_from) // 4 : (t1 - plane_from) // 4].bitcast(U8),
+                )
+
+            if c0 < TURNED:
+                for i in range(HALF // P):
+                    t_codes, t_scales = table(c0 + i * P, c0 + (i + 1) * P)
+                    nc.tensor.matmul_mx(
+                        out=sums[g][:, i * P : (i + 1) * P],
+                        lhsT=t_codes,
+                        lhsT_scale=t_scales,
+                        rhs=codes,
+                        rhs_scale=scales,
+                        start=(a == 0 and i == 0),
+                        stop=(a == PASSES - 1 and i == HALF // P - 1),
+                    )
+            else:
+                t_codes, t_scales = table(c0, c0 + HALF)
+                nc.tensor.matmul_mx(
+                    out=sums[g][:],
+                    lhsT=codes,
+                    lhsT_scale=scales,
+                    rhs=t_codes,
+                    rhs_scale=t_scales,
+                    start=(a == 0),
+                    stop=(a == PASSES - 1),
+                )
+
+        def gather_pass2(c0, words):
+            c1 = c0 + words.shape[1]
+            nc.vector.tensor_copy(words, window2[:].bitcast(U32).indirect(offsets[:, c0 // 16 : c1 // 16]))
             return words
 
         quantize_w(0, 2, w_bf16_early[:].rearrange("p a c -> p (a c)"))
-        for g in range(len(ranges)):
-            multiply(0, g, picked[0], 0)
-        multiply(1, 0, picked[1], 0)
-        head = gather_pass2(0, 2 * N, tile([P, 2 * N], U32, "picked_head"))
+        for a in range(2):
+            for g in range(len(starts)):
+                multiply(a, g, picked[a], 0, planes[a], 0)
+
+        scaled = [tile([P, HALF], F32, f"scaled{g}") for g in range(len(starts))]
+        result = [tile([P, HALF], F32, f"result{g}") for g in range(len(starts))]
+        range_bytes = 4 * HALF
+        scaled1_at = w_last_end + 4 * N + range_bytes - 128
+        scaled[1] = late_tile([P, HALF], F32, "scaled_held", scaled1_at)
+        result[2] = late_tile([P, HALF], F32, "result_below", scaled1_at + 64 - range_bytes)
+        result[3] = late_tile([P, HALF], F32, "result_above", scaled1_at + range_bytes - 64)
+
+        def scale_turned(g):
+            for i in range(HALF // P):
+                c0 = starts[g] + i * P
+                nc.scalar.activation(
+                    scaled[g][:, i * P : (i + 1) * P],
+                    sums[g][:, i * P : (i + 1) * P],
+                    IDENTITY,
+                    scale=ts_columns[:, c0 // P : c0 // P + 1],
+                )
+
+        def turn_back(g):
+            c0 = starts[g]
+            back = flip_pool.tile([P, HALF], F32, name="back", tag="flip")
+            for i in range(HALF // P):
+                nc.tensor.transpose(back[:, i * P : (i + 1) * P], scaled[g][:, i * P : (i + 1) * P], identity[:])
+            nc.scalar.activation(result[g][:], back[:], IDENTITY, bias=bias[:])
+            nc.sync.dma_start(out[:, c0 : c0 + HALF], result[g][:])
+
+        first = gather_pass2(0, tile([P, N], U32, "picked_first")[:])
         quantize_w(2, 3, w_bf16_last[:])
         for g in (0, 1):
-            multiply(2, g, head, 0)
-        multiply(1, 1, picked[1], 0)
-        tail = gather_pass2(
-            2 * N, S, late.tile([P, N], U32, name="picked_tail", offset=word_window_bytes, align_bytes=64)
-        )
+            multiply(2, g, first, 0, planes[2], 0)
+        second = gather_pass2(N, late_tile([P, N], U32, "picked_second", w_last_at + 64 - 4 * N)[:])
         for g in (2, 3):
-            multiply(2, g, tail, 2 * N)
-            multiply(1, g, picked[1], 0)
+            multiply(2, g, second, N, planes[2], 0)
+        for g in range(TURNED // HALF):
+            scale_turned(g)
+        for g in range(TURNED // HALF):
+            turn_back(g)
+        third = late_tile([P, N], U32, "picked_third", w_last_end - 64)
+        for g in (4, 5):
+            gather_pass2(starts[g], third[:, starts[g] - 2 * N : starts[g] - 2 * N + HALF])
+            multiply(2, g, third, 2 * N, plane_last, 2 * N)
 
-        scaled = tile([P, S], F32, "scaled")
-        result = tile([P, S], F32, "result")
-
-        def scale(g, c0, c1):
-            sum_from = ranges[g][0]
+        def scale(g):
+            c0 = starts[g]
             nc.vector.tensor_tensor(
-                scaled[:, c0:c1], sums[g][:, c0 - sum_from : c1 - sum_from], ts_spread[:, c0:c1], MULT
+                scaled[g][:], sums[g][:], ts_spread[:, c0 - TURNED : c0 - TURNED + HALF], MULT
             )
 
-        cuts = (0, P, HALF, N, N + HALF, 2 * N)
-        for c0, c1 in zip(cuts, cuts[1:]):
-            scale(c0 // N, c0, c1)
-            nc.scalar.activation(result[:, c0:c1], scaled[:, c0:c1], IDENTITY, bias=bias[:])
-            nc.sync.dma_start(out[:, c0:c1], result[:, c0:c1])
-        for g in (2, 3):
-            scale(g, *ranges[g])
-        for c0, c1 in ranges[2:]:
-            nc.vector.tensor_scalar_add(result[:, c0:c1], scaled[:, c0:c1], bias[:])
-            nc.sync.dma_start(out[:, c0:c1], result[:, c0:c1])
+        for g in range(TURNED // HALF, 4):
+            c0, c1 = starts[g], starts[g] + HALF
+            scale(g)
+            nc.scalar.activation(result[g][:], scaled[g][:], IDENTITY, bias=bias[:])
+            nc.sync.dma_start(out[:, c0:c1], result[g][:])
+        for g in (4, 5):
+            scale(g)
+        for g in (4, 5):
+            c0, c1 = starts[g], starts[g] + HALF
+            nc.vector.tensor_scalar_add(result[g][:], scaled[g][:], bias[:])
+            nc.sync.dma_start(out[:, c0:c1], result[g][:])

@@ -29,7 +29,7 @@ BLOCKS = N // P
 LIVE_ROW = P - 1
 SCALE_FIRST = 3 * QUADRANT - PASSES * SCALE_ROWS
 SCALE_END = 3 * QUADRANT
-TS_ZEROED_BY_VECTOR = 768
+TS_ZEROED_BY_VECTOR = 640
 TURNED = 512
 
 
@@ -39,7 +39,6 @@ def tile_list_tabts_bias_kernel(tc, tab_words, tab_scales, w, ts, b, offs, out):
         keep = ctx.enter_context(tc.tile_pool(name="keep", bufs=1))
         late = ctx.enter_context(tc.tile_pool(name="late", bufs=1))
         acc_pool = ctx.enter_context(tc.psum_pool(name="acc", bufs=1))
-        flip_pool = ctx.enter_context(tc.psum_pool(name="flip", bufs=2))
 
         def tile(shape, dtype, name, slot=None):
             return keep.tile(shape, dtype, name=name, tag=slot or name, align_bytes=64)
@@ -49,7 +48,6 @@ def tile_list_tabts_bias_kernel(tc, tab_words, tab_scales, w, ts, b, offs, out):
                 nc.vector.memset(rows[:, c0:c1], 0)
 
         offsets = keep.tile([P, S // 16], U16, name="offsets")
-        nc.sync.dma_start(offsets[:], offs)
 
         def late_tile(shape, dtype, name, offset):
             return late.tile(shape, dtype, name=name, offset=offset, align_bytes=64)
@@ -64,13 +62,15 @@ def tile_list_tabts_bias_kernel(tc, tab_words, tab_scales, w, ts, b, offs, out):
                 scale_window[SCALE_FIRST + a : SCALE_END : PASSES, :],
                 scale_rows[a * SCALE_ROWS : (a + 1) * SCALE_ROWS, :],
             )
+        nc.sync.dma_start(offsets[:], offs)
         zero_on_vector(scale_window[0:SCALE_FIRST, :], T // 4)
         nc.gpsimd.memset(scale_window[SCALE_END:P, :], 0)
 
-        planes = [tile([P, S // 4], I32, f"planes{a}") for a in range(2)]
-        planes.append(tile([P, 2 * N // 4], I32, "planes2"))
-        for plane in planes[:2]:
-            nc.gpsimd.memset(plane[:], 0)
+        rounded_at = w_last_end + 8 * N + 6 * N
+        rounded_bytes = 2 * 2 * M * PACK
+        planes_early = tile([P, S // 4], I32, "planes_early")
+        nc.gpsimd.memset(planes_early[:], 0)
+        planes = [planes_early, planes_early, late_tile([P, 2 * N // 4], I32, "planes2", rounded_at + 64 - 2 * N)]
 
         w_rows = w.rearrange("(a p i) n -> p a (i n)", p=P, i=PACK)
         w_raw_early = tile([P, 2, PACK * M], F32, "w_raw_early")
@@ -82,14 +82,14 @@ def tile_list_tabts_bias_kernel(tc, tab_words, tab_scales, w, ts, b, offs, out):
         nc.gpsimd.memset(ts_window[0:LIVE_ROW, TS_ZEROED_BY_VECTOR:T], 0.0)
 
         bias_row = tile([P, P], F32, "bias_row")
-        nc.scalar.dma_start(bias_row[LIVE_ROW:P, :], b.rearrange("(o n) -> o n", o=1))
-        nc.gpsimd.memset(bias_row[0:LIVE_ROW, :], 0.0)
+        nc.sync.dma_start(bias_row[LIVE_ROW:P, :], b.rearrange("(o n) -> o n", o=1))
+        zero_on_vector(bias_row[0:LIVE_ROW, :], P)
 
         def load_words(a, window):
             nc.sync.dma_start(window[:], tab_words[a].rearrange("p t i -> p (t i)").bitcast(I32))
             return window
 
-        w_bf16_early = tile([P, 2, M * PACK], BF16, "w_bf16_early")
+        w_bf16_early = late_tile([P, 2, M * PACK], BF16, "w_bf16_early", rounded_at)
         w_bf16_last = tile([P, M * PACK], BF16, "w_bf16_last")
 
         def round_w(rounded, raw):
@@ -103,7 +103,7 @@ def tile_list_tabts_bias_kernel(tc, tab_words, tab_scales, w, ts, b, offs, out):
             round_w(w_bf16_early[:, a, :], w_raw_early[:, a, :])
         window1 = load_words(1, tile([P, T], I32, "word_window1"))
 
-        identity = tile([P, P], F32, "identity")
+        identity = late_tile([P, P], F32, "identity", rounded_at + rounded_bytes - 64)
         make_identity(nc, identity[:])
         nc.gpsimd.memset(planes[2][:], 0)
 
@@ -128,29 +128,32 @@ def tile_list_tabts_bias_kernel(tc, tab_words, tab_scales, w, ts, b, offs, out):
         nc.sync.dma_start(w_raw_last[:], w_rows[:, 2, :])
         place_scales(2, planes[2], 0, 2 * N)
         round_w(w_bf16_last[:], w_raw_last[:])
-        plane_last = tile([P, N // 4], I32, "plane_last")
+        plane_last = late_tile([P, N // 4], I32, "plane_last", rounded_at + 256)
         nc.gpsimd.memset(plane_last[:], 0)
         place_scales(2, plane_last, 2 * N, S)
 
         ts_picked = tile([P, S], F32, "ts_picked")
         nc.vector.tensor_copy(ts_picked[:], ts_window[:].indirect(offsets[:]))
 
+        def early_bank(shape, turn):
+            return acc_pool.tile(shape, F32, name="early", tag=f"sum{5 + turn % 2}")
+
         ts_columns = tile([P, SLICES * BLOCKS], F32, "ts_columns")
         ts_spread = tile([P, S - TURNED], F32, "ts_spread")
         for s in range(SLICES):
-            turned = flip_pool.tile([P, BLOCKS, P], F32, name="turned", tag="flip")
+            turned = early_bank([P, BLOCKS, P], s)
             for i in range(BLOCKS):
                 c0 = s * N + i * P
                 nc.tensor.transpose(turned[:, i, :], ts_picked[:, c0 : c0 + P], identity[:])
             nc.scalar.copy(ts_columns[:, s * BLOCKS : (s + 1) * BLOCKS], turned[:, :, LIVE_ROW])
 
         bias = tile([P, 1], F32, "bias")
-        turned = flip_pool.tile([P, BLOCKS, P], F32, name="turned", tag="flip")
+        turned = early_bank([P, BLOCKS, P], SLICES)
         nc.tensor.transpose(turned[:, 0, :], bias_row[:], identity[:])
         nc.scalar.copy(bias[:], turned[:, 0, LIVE_ROW:P])
 
         for c0 in range(TURNED, S, HALF):
-            spread = flip_pool.tile([P, HALF], F32, name="spread", tag="flip")
+            spread = early_bank([P, HALF], c0 // HALF + 1)
             for i in range(HALF // P):
                 column = c0 // P + i
                 nc.tensor.transpose(
@@ -166,15 +169,16 @@ def tile_list_tabts_bias_kernel(tc, tab_words, tab_scales, w, ts, b, offs, out):
 
         w_codes = tile([P, PASSES * M], U32, "w_codes")
         w_scales = tile([P, PASSES * M], U8, "w_scales")
-        starts = range(0, S, HALF)
-        sums = [acc_pool.tile([P, HALF], F32, name=f"sum{g}") for g in range(len(starts))]
+        starts = list(range(0, S, HALF)) + [S - P]
+        widths = [c1 - c0 for c0, c1 in zip(starts, starts[1:] + [S])]
+        sums = [acc_pool.tile([P, n], F32, name=f"sum{g}", tag=f"sum{g}") for g, n in enumerate(widths)]
 
         def quantize_w(a0, a1, rounded):
             nc.vector.quantize_mx(
                 out=w_codes[:, a0 * M : a1 * M].bitcast(FP8X4), scales=w_scales[:, a0 * M : a1 * M], in_=rounded
             )
 
-        def multiply(a, g, words, words_from, plane, plane_from):
+        def multiply(a, g, words, words_from, plane, plane_from, part=None):
             c0 = starts[g]
             codes, scales = w_codes[:, a * M : (a + 1) * M].bitcast(FP8X4), w_scales[:, a * M : (a + 1) * M]
 
@@ -197,15 +201,16 @@ def tile_list_tabts_bias_kernel(tc, tab_words, tab_scales, w, ts, b, offs, out):
                         stop=(a == PASSES - 1 and i == HALF // P - 1),
                     )
             else:
-                t_codes, t_scales = table(c0, c0 + HALF)
+                p0, p1 = part or (0, widths[g])
+                t_codes, t_scales = table(c0 + p0, c0 + p1)
                 nc.tensor.matmul_mx(
-                    out=sums[g][:],
+                    out=sums[g][:, p0:p1],
                     lhsT=codes,
                     lhsT_scale=scales,
                     rhs=t_codes,
                     rhs_scale=t_scales,
                     start=(a == 0),
-                    stop=(a == PASSES - 1),
+                    stop=(a == PASSES - 1 and p1 == widths[g]),
                 )
 
         def gather_pass2(c0, words):
@@ -218,8 +223,8 @@ def tile_list_tabts_bias_kernel(tc, tab_words, tab_scales, w, ts, b, offs, out):
             for g in range(len(starts)):
                 multiply(a, g, picked[a], 0, planes[a], 0)
 
-        scaled = [tile([P, HALF], F32, f"scaled{g}") for g in range(len(starts))]
-        result = [tile([P, HALF], F32, f"result{g}") for g in range(len(starts))]
+        scaled = [tile([P, n], F32, f"scaled{g}") for g, n in enumerate(widths)]
+        result = [tile([P, HALF], F32, f"result{g}") for g in range(S // HALF)]
         range_bytes = 4 * HALF
         scaled1_at = w_last_end + 4 * N + range_bytes - 128
         scaled[1] = late_tile([P, HALF], F32, "scaled_held", scaled1_at)
@@ -238,19 +243,20 @@ def tile_list_tabts_bias_kernel(tc, tab_words, tab_scales, w, ts, b, offs, out):
 
         def turn_back(g):
             c0 = starts[g]
-            back = flip_pool.tile([P, HALF], F32, name="back", tag="flip")
+            back = acc_pool.tile([P, HALF], F32, name="back", tag=("back", "sum0")[g])
             for i in range(HALF // P):
                 nc.tensor.transpose(back[:, i * P : (i + 1) * P], scaled[g][:, i * P : (i + 1) * P], identity[:])
             nc.scalar.activation(result[g][:], back[:], IDENTITY, bias=bias[:])
             nc.sync.dma_start(out[:, c0 : c0 + HALF], result[g][:])
 
-        first = gather_pass2(0, tile([P, N], U32, "picked_first")[:])
+        first = gather_pass2(0, tile([P, N + P], U32, "picked_first")[:])
         quantize_w(2, 3, w_bf16_last[:])
         for g in (0, 1):
             multiply(2, g, first, 0, planes[2], 0)
-        second = gather_pass2(N, late_tile([P, N], U32, "picked_second", w_last_at + 64 - 4 * N)[:])
-        for g in (2, 3):
-            multiply(2, g, second, N, planes[2], 0)
+        multiply(2, 2, first, 0, planes[2], 0, (0, P))
+        second = gather_pass2(N + P, late_tile([P, N - P], U32, "picked_second", w_last_at + 64 - 4 * (N - P))[:])
+        multiply(2, 2, second, N + P, planes[2], 0, (P, HALF))
+        multiply(2, 3, second, N + P, planes[2], 0)
         for g in range(TURNED // HALF):
             scale_turned(g)
         for g in range(TURNED // HALF):
@@ -259,21 +265,23 @@ def tile_list_tabts_bias_kernel(tc, tab_words, tab_scales, w, ts, b, offs, out):
         for g in (4, 5):
             gather_pass2(starts[g], third[:, starts[g] - 2 * N : starts[g] - 2 * N + HALF])
             multiply(2, g, third, 2 * N, plane_last, 2 * N)
+        multiply(2, 6, third, 2 * N, plane_last, 2 * N)
 
-        def scale(g):
-            c0 = starts[g]
-            nc.vector.tensor_tensor(
-                scaled[g][:], sums[g][:], ts_spread[:, c0 - TURNED : c0 - TURNED + HALF], MULT
-            )
+        def scale(g, c0=0, c1=None):
+            c1 = c1 or widths[g]
+            at = starts[g] - TURNED
+            nc.vector.tensor_tensor(scaled[g][:, c0:c1], sums[g][:, c0:c1], ts_spread[:, at + c0 : at + c1], MULT)
 
-        for g in range(TURNED // HALF, 4):
-            c0, c1 = starts[g], starts[g] + HALF
-            scale(g)
-            nc.scalar.activation(result[g][:], scaled[g][:], IDENTITY, bias=bias[:])
-            nc.sync.dma_start(out[:, c0:c1], result[g][:])
-        for g in (4, 5):
-            scale(g)
-        for g in (4, 5):
-            c0, c1 = starts[g], starts[g] + HALF
-            nc.vector.tensor_scalar_add(result[g][:], scaled[g][:], bias[:])
-            nc.sync.dma_start(out[:, c0:c1], result[g][:])
+        for g, c0, c1 in ((2, 0, P), (2, P, HALF), (3, 0, HALF)):
+            scale(g, c0, c1)
+            nc.scalar.activation(result[g][:, c0:c1], scaled[g][:, c0:c1], IDENTITY, bias=bias[:])
+            nc.sync.dma_start(out[:, starts[g] + c0 : starts[g] + c1], result[g][:, c0:c1])
+        scale(4)
+        scale(5)
+        nc.vector.tensor_scalar_add(result[4][:], scaled[4][:], bias[:])
+        nc.sync.dma_start(out[:, starts[4] : starts[5]], result[4][:])
+        scale(6)
+        for g in (5, 6):
+            c0 = starts[g] - starts[5]
+            nc.vector.tensor_scalar_add(result[5][:, c0 : c0 + P], scaled[g][:], bias[:])
+        nc.sync.dma_start(out[:, starts[5] : S], result[5][:])

@@ -30,7 +30,7 @@ LIVE_ROW = P - 1
 SCALE_FIRST = 3 * QUADRANT - PASSES * SCALE_ROWS
 SCALE_END = 3 * QUADRANT
 TS_ZEROED_BY_VECTOR = 640
-TURNED = 512
+TURNED = 640
 
 
 def tile_list_tabts_bias_kernel(tc, tab_words, tab_scales, w, ts, b, offs, out):
@@ -152,16 +152,17 @@ def tile_list_tabts_bias_kernel(tc, tab_words, tab_scales, w, ts, b, offs, out):
         nc.tensor.transpose(turned[:, 0, :], bias_row[:], identity[:])
         nc.scalar.copy(bias[:], turned[:, 0, LIVE_ROW:P])
 
-        for c0 in range(TURNED, S, HALF):
-            spread = early_bank([P, HALF], c0 // HALF + 1)
-            for i in range(HALF // P):
+        for turn, c0 in enumerate(range(TURNED, S, N)):
+            width = min(N, S - c0)
+            spread = early_bank([P, width], turn)
+            for i in range(width // P):
                 column = c0 // P + i
                 nc.tensor.transpose(
                     spread[:, i * P : (i + 1) * P],
                     ts_columns[:, column : column + 1].to_broadcast([P, P]),
                     identity[:],
                 )
-            nc.scalar.copy(ts_spread[:, c0 - TURNED : c0 - TURNED + HALF], spread[:])
+            nc.scalar.copy(ts_spread[:, c0 - TURNED : c0 - TURNED + width], spread[:])
 
         picked = [tile([P, S], U32, "picked0"), tile([P, S], U32, "picked1")]
         nc.vector.tensor_copy(picked[0][:], window0[:].bitcast(U32).indirect(offsets[:]))
@@ -169,7 +170,7 @@ def tile_list_tabts_bias_kernel(tc, tab_words, tab_scales, w, ts, b, offs, out):
 
         w_codes = tile([P, PASSES * M], U32, "w_codes")
         w_scales = tile([P, PASSES * M], U8, "w_scales")
-        starts = list(range(0, S, HALF)) + [S - P]
+        starts = [0, HALF, N, TURNED, 2 * N, S - HALF, S - P]
         widths = [c1 - c0 for c0, c1 in zip(starts, starts[1:] + [S])]
         sums = [acc_pool.tile([P, n], F32, name=f"sum{g}", tag=f"sum{g}") for g, n in enumerate(widths)]
 
@@ -178,7 +179,7 @@ def tile_list_tabts_bias_kernel(tc, tab_words, tab_scales, w, ts, b, offs, out):
                 out=w_codes[:, a0 * M : a1 * M].bitcast(FP8X4), scales=w_scales[:, a0 * M : a1 * M], in_=rounded
             )
 
-        def multiply(a, g, words, words_from, plane, plane_from, part=None):
+        def multiply(a, g, words, words_from, plane, plane_from):
             c0 = starts[g]
             codes, scales = w_codes[:, a * M : (a + 1) * M].bitcast(FP8X4), w_scales[:, a * M : (a + 1) * M]
 
@@ -189,7 +190,7 @@ def tile_list_tabts_bias_kernel(tc, tab_words, tab_scales, w, ts, b, offs, out):
                 )
 
             if c0 < TURNED:
-                for i in range(HALF // P):
+                for i in range(widths[g] // P):
                     t_codes, t_scales = table(c0 + i * P, c0 + (i + 1) * P)
                     nc.tensor.matmul_mx(
                         out=sums[g][:, i * P : (i + 1) * P],
@@ -198,20 +199,22 @@ def tile_list_tabts_bias_kernel(tc, tab_words, tab_scales, w, ts, b, offs, out):
                         rhs=codes,
                         rhs_scale=scales,
                         start=(a == 0 and i == 0),
-                        stop=(a == PASSES - 1 and i == HALF // P - 1),
+                        stop=(a == PASSES - 1 and i == widths[g] // P - 1),
                     )
             else:
-                p0, p1 = part or (0, widths[g])
-                t_codes, t_scales = table(c0 + p0, c0 + p1)
-                nc.tensor.matmul_mx(
-                    out=sums[g][:, p0:p1],
-                    lhsT=codes,
-                    lhsT_scale=scales,
-                    rhs=t_codes,
-                    rhs_scale=t_scales,
-                    start=(a == 0),
-                    stop=(a == PASSES - 1 and p1 == widths[g]),
-                )
+                odd = widths[g] % HALF if widths[g] > HALF else 0
+                for p0, p1 in ((0, odd), (odd, widths[g])):
+                    if p1 > p0:
+                        t_codes, t_scales = table(c0 + p0, c0 + p1)
+                        nc.tensor.matmul_mx(
+                            out=sums[g][:, p0:p1],
+                            lhsT=codes,
+                            lhsT_scale=scales,
+                            rhs=t_codes,
+                            rhs_scale=t_scales,
+                            start=(a == 0 and p0 == 0),
+                            stop=(a == PASSES - 1 and p1 == widths[g]),
+                        )
 
         def gather_pass2(c0, words):
             c1 = c0 + words.shape[1]
@@ -223,16 +226,16 @@ def tile_list_tabts_bias_kernel(tc, tab_words, tab_scales, w, ts, b, offs, out):
             for g in range(len(starts)):
                 multiply(a, g, picked[a], 0, planes[a], 0)
 
-        scaled = [tile([P, n], F32, f"scaled{g}") for g, n in enumerate(widths)]
-        result = [tile([P, HALF], F32, f"result{g}") for g in range(S // HALF)]
-        range_bytes = 4 * HALF
-        scaled1_at = w_last_end + 4 * N + range_bytes - 128
-        scaled[1] = late_tile([P, HALF], F32, "scaled_held", scaled1_at)
-        result[2] = late_tile([P, HALF], F32, "result_below", scaled1_at + 64 - range_bytes)
-        result[3] = late_tile([P, HALF], F32, "result_above", scaled1_at + range_bytes - 64)
+        scaled1_at = w_last_end + 4 * N
+        scaled = [tile([P, n], F32, f"scaled{g}") for g, n in enumerate(widths[:5])]
+        scaled[2] = late_tile([P, widths[2]], F32, "scaled_held", scaled1_at)
+        scaled_last = tile([P, HALF], F32, "scaled_last")
+        scaled[5:] = [scaled_last[:, 0:P], scaled_last[:, P:HALF]]
+        result = [tile([P, n], F32, f"result{g}") for g, n in enumerate(widths[:5] + [HALF])]
+        result[3] = late_tile([P, widths[3]], F32, "result_above", scaled1_at + 4 * widths[2] - 64)
 
         def scale_turned(g):
-            for i in range(HALF // P):
+            for i in range(widths[g] // P):
                 c0 = starts[g] + i * P
                 nc.scalar.activation(
                     scaled[g][:, i * P : (i + 1) * P],
@@ -243,45 +246,39 @@ def tile_list_tabts_bias_kernel(tc, tab_words, tab_scales, w, ts, b, offs, out):
 
         def turn_back(g):
             c0 = starts[g]
-            back = acc_pool.tile([P, HALF], F32, name="back", tag=("back", "sum0")[g])
-            for i in range(HALF // P):
+            back = acc_pool.tile([P, widths[g]], F32, name="back", tag=("back", "sum0", "sum1")[g])
+            for i in range(widths[g] // P):
                 nc.tensor.transpose(back[:, i * P : (i + 1) * P], scaled[g][:, i * P : (i + 1) * P], identity[:])
             nc.scalar.activation(result[g][:], back[:], IDENTITY, bias=bias[:])
-            nc.sync.dma_start(out[:, c0 : c0 + HALF], result[g][:])
+            nc.sync.dma_start(out[:, c0 : c0 + widths[g]], result[g][:])
 
-        first = gather_pass2(0, tile([P, N + P], U32, "picked_first")[:])
+        first = gather_pass2(0, tile([P, TURNED], U32, "picked_first")[:])
         quantize_w(2, 3, w_bf16_last[:])
-        for g in (0, 1):
+        for g in (0, 1, 2):
             multiply(2, g, first, 0, planes[2], 0)
-        multiply(2, 2, first, 0, planes[2], 0, (0, P))
-        second = gather_pass2(N + P, late_tile([P, N - P], U32, "picked_second", w_last_at + 64 - 4 * (N - P))[:])
-        multiply(2, 2, second, N + P, planes[2], 0, (P, HALF))
-        multiply(2, 3, second, N + P, planes[2], 0)
-        for g in range(TURNED // HALF):
+        second = gather_pass2(TURNED, late_tile([P, widths[3]], U32, "picked_second", w_last_at + 64 - 4 * widths[3])[:])
+        multiply(2, 3, second, TURNED, planes[2], 0)
+        for g in (0, 1, 2):
             scale_turned(g)
-        for g in range(TURNED // HALF):
+        for g in (0, 1, 2):
             turn_back(g)
         third = late_tile([P, N], U32, "picked_third", w_last_end - 64)
-        for g in (4, 5):
-            gather_pass2(starts[g], third[:, starts[g] - 2 * N : starts[g] - 2 * N + HALF])
+        for h in range(2):
+            gather_pass2(2 * N + h * HALF, third[:, h * HALF : (h + 1) * HALF])
+        for g in (4, 5, 6):
             multiply(2, g, third, 2 * N, plane_last, 2 * N)
-        multiply(2, 6, third, 2 * N, plane_last, 2 * N)
 
         def scale(g, c0=0, c1=None):
             c1 = c1 or widths[g]
             at = starts[g] - TURNED
             nc.vector.tensor_tensor(scaled[g][:, c0:c1], sums[g][:, c0:c1], ts_spread[:, at + c0 : at + c1], MULT)
 
-        for g, c0, c1 in ((2, 0, P), (2, P, HALF), (3, 0, HALF)):
-            scale(g, c0, c1)
-            nc.scalar.activation(result[g][:, c0:c1], scaled[g][:, c0:c1], IDENTITY, bias=bias[:])
-            nc.sync.dma_start(out[:, starts[g] + c0 : starts[g] + c1], result[g][:, c0:c1])
-        scale(4)
-        scale(5)
-        nc.vector.tensor_scalar_add(result[4][:], scaled[4][:], bias[:])
-        nc.sync.dma_start(out[:, starts[4] : starts[5]], result[4][:])
-        scale(6)
-        for g in (5, 6):
-            c0 = starts[g] - starts[5]
-            nc.vector.tensor_scalar_add(result[5][:, c0 : c0 + P], scaled[g][:], bias[:])
-        nc.sync.dma_start(out[:, starts[5] : S], result[5][:])
+        for c0, c1 in ((0, P), (P, widths[3])):
+            scale(3, c0, c1)
+            nc.scalar.activation(result[3][:, c0:c1], scaled[3][:, c0:c1], IDENTITY, bias=bias[:])
+            nc.sync.dma_start(out[:, starts[3] + c0 : starts[3] + c1], result[3][:, c0:c1])
+        for g in (4, 5, 6):
+            scale(g)
+        for g, products in ((4, scaled[4]), (5, scaled_last)):
+            nc.vector.tensor_scalar_add(result[g][:], products[:], bias[:])
+            nc.sync.dma_start(out[:, starts[g] : starts[g] + HALF], result[g][:])

@@ -170,7 +170,7 @@ def tile_list_tabts_bias_kernel(tc, tab_words, tab_scales, w, ts, b, offs, out):
 
         w_codes = tile([P, PASSES * M], U32, "w_codes")
         w_scales = tile([P, PASSES * M], U8, "w_scales")
-        starts = [0, HALF, N, TURNED, 2 * N, S - HALF, S - P]
+        starts = [0, P, P + HALF, TURNED, 2 * N, S - HALF, S - P]
         widths = [c1 - c0 for c0, c1 in zip(starts, starts[1:] + [S])]
         sums = [acc_pool.tile([P, n], F32, name=f"sum{g}", tag=f"sum{g}") for g, n in enumerate(widths)]
 
@@ -279,6 +279,9 @@ def tile_list_tabts_bias_kernel(tc, tab_words, tab_scales, w, ts, b, offs, out):
             nc.sync.dma_start(out[:, starts[3] + c0 : starts[3] + c1], result[3][:, c0:c1])
         for g in (4, 5, 6):
             scale(g)
-        for g, products in ((4, scaled[4]), (5, scaled_last)):
-            nc.vector.tensor_scalar_add(result[g][:], products[:], bias[:])
-            nc.sync.dma_start(out[:, starts[g] : starts[g] + HALF], result[g][:])
+        nc.vector.tensor_scalar_add(result[4][:], scaled[4][:], bias[:])
+        nc.sync.dma_start(out[:, starts[4] : starts[5]], result[4][:])
+        for g in (5, 6):
+            c0 = starts[g] - starts[5]
+            nc.vector.tensor_scalar_add(result[5][:, c0 : c0 + P], scaled[g], bias[:])
+        nc.sync.dma_start(out[:, starts[5] : S], result[5][:])

from contextlib import ExitStack

import concourse.mybir as mybir
from concourse.masks import make_identity

K, M, T, S = 1536, 128, 4096, 1536
FLOPS = 2 * K * M * S
BYTES = K * T + (K // 32) * T + 4 * K * M + 4 * T + 4 * M + 2 * 128 * (S // 16) + 4 * M * S

F32 = mybir.dt.float32
BF16 = mybir.dt.bfloat16
I32 = mybir.dt.int32
U32 = mybir.dt.uint32
U16 = mybir.dt.uint16
U8 = mybir.dt.uint8
FP8X4 = mybir.dt.float8_e4m3fn_x4
MULT = mybir.AluOpType.mult
IDENTITY = mybir.ActivationFunctionType.Identity

P = 128
QUADRANT = 32
PACK = 4
PASSES = K // (P * PACK)
SCALE_ROWS = 16
N = 512
HALF = N // 2
SLICES = S // N
BLOCKS = N // P
LIVE_ROW = P - 1
SCALE_FIRST = 3 * QUADRANT - PASSES * SCALE_ROWS
SCALE_END = 3 * QUADRANT
TS_ZEROED_BY_VECTOR = 640
TURNED = 640


def tile_list_tabts_bias_kernel(tc, tab_words, tab_scales, w, ts, b, offs, out):
    nc = tc.nc
    with ExitStack() as ctx:
        keep = ctx.enter_context(tc.tile_pool(name="keep", bufs=1))
        late = ctx.enter_context(tc.tile_pool(name="late", bufs=1))
        acc_pool = ctx.enter_context(tc.psum_pool(name="acc", bufs=1))

        def tile(shape, dtype, name, slot=None):
            return keep.tile(shape, dtype, name=name, tag=slot or name, align_bytes=64)

        def zero_on_vector(rows, columns):
            for c0, c1 in ((0, columns - 1), (columns - 1, columns)):
                nc.vector.memset(rows[:, c0:c1], 0)

        offsets = keep.tile([P, S // 16], U16, name="offsets")

        def late_tile(shape, dtype, name, offset):
            return late.tile(shape, dtype, name=name, offset=offset, align_bytes=64)

        window_bytes = 4 * T
        w_last_at = window_bytes + 4 * N
        w_last_end = w_last_at + 4 * PACK * M
        scale_rows = tab_scales.rearrange("a q t -> (a q) t").bitcast(I32)
        scale_window = late_tile([P, T // 4], I32, "scale_window", window_bytes - 64)
        for a in range(PASSES):
            nc.sync.dma_start(
                scale_window[SCALE_FIRST + a : SCALE_END : PASSES, :],
                scale_rows[a * SCALE_ROWS : (a + 1) * SCALE_ROWS, :],
            )
        nc.sync.dma_start(offsets[:], offs)
        zero_on_vector(scale_window[0:SCALE_FIRST, :], T // 4)
        nc.gpsimd.memset(scale_window[SCALE_END:P, :], 0)

        rounded_at = w_last_end + 8 * N + 6 * N
        rounded_bytes = 2 * 2 * M * PACK
        planes_early = tile([P, S // 4], I32, "planes_early")
        nc.gpsimd.memset(planes_early[:], 0)
        planes = [planes_early, planes_early, late_tile([P, 2 * N // 4], I32, "planes2", rounded_at + 64 - 2 * N)]

        w_rows = w.rearrange("(a p i) n -> p a (i n)", p=P, i=PACK)
        w_raw_early = tile([P, 2, PACK * M], F32, "w_raw_early")
        nc.sync.dma_start(w_raw_early[:], w_rows[:, 0:2, :])

        ts_window = tile([P, T], F32, "ts_window")
        nc.sync.dma_start(ts_window[LIVE_ROW:P, :], ts[0:1, :])
        zero_on_vector(ts_window[0:LIVE_ROW, :], TS_ZEROED_BY_VECTOR)
        nc.gpsimd.memset(ts_window[0:LIVE_ROW, TS_ZEROED_BY_VECTOR:T], 0.0)

        bias_row = tile([P, P], F32, "bias_row")
        nc.sync.dma_start(bias_row[LIVE_ROW:P, :], b.rearrange("(o n) -> o n", o=1))
        zero_on_vector(bias_row[0:LIVE_ROW, :], P)

        def load_words(a, window):
            nc.sync.dma_start(window[:], tab_words[a].rearrange("p t i -> p (t i)").bitcast(I32))
            return window

        w_bf16_early = late_tile([P, 2, M * PACK], BF16, "w_bf16_early", rounded_at)
        w_bf16_last = tile([P, M * PACK], BF16, "w_bf16_last")

        def round_w(rounded, raw):
            nc.scalar.copy(
                rounded.rearrange("p (c j i) -> p c i j", j=4, i=PACK),
                raw.rearrange("p (i c j) -> p c i j", i=PACK, j=4),
            )

        window0 = load_words(0, tile([P, T], I32, "word_window0"))
        for a in range(2):
            round_w(w_bf16_early[:, a, :], w_raw_early[:, a, :])
        window1 = load_words(1, tile([P, T], I32, "word_window1"))

        identity = late_tile([P, P], F32, "identity", rounded_at + rounded_bytes - 64)
        make_identity(nc, identity[:])
        nc.gpsimd.memset(planes[2][:], 0)

        scales_picked = tile([P, S], U8, "scales_picked")
        nc.vector.tensor_copy(scales_picked[:], scale_window[:].bitcast(U8).indirect(offsets[:]))

        def place_scales(a, plane, c0, c1):
            for r in range(4):
                first = SCALE_FIRST + PASSES * r + a
                nc.sync.dma_start(
                    plane[4 * a + r : P : QUADRANT, :],
                    scales_picked[first:SCALE_END : 4 * PASSES, c0:c1].bitcast(I32),
                )

        place_scales(0, planes[0], 0, S)
        window2 = late_tile([P, T], I32, "word_window2", 0)
        words2 = tab_words[2].rearrange("p t i -> p (t i)").bitcast(I32)
        nc.sync.dma_start(window2[:, 0 : T // 2], words2[:, 0 : T // 2])
        place_scales(1, planes[1], 0, S)
        nc.sync.dma_start(window2[:, T // 2 : T], words2[:, T // 2 : T])
        w_raw_last = late_tile([P, PACK * M], F32, "w_raw_last", w_last_at)
        nc.sync.dma_start(w_raw_last[:], w_rows[:, 2, :])
        place_scales(2, planes[2], 0, 2 * N)
        round_w(w_bf16_last[:], w_raw_last[:])
        plane_last = late_tile([P, N // 4], I32, "plane_last", rounded_at + 256)
        nc.gpsimd.memset(plane_last[:], 0)
        place_scales(2, plane_last, 2 * N, S)

        ts_picked = tile([P, S], F32, "ts_picked")
        nc.vector.tensor_copy(ts_picked[:], ts_window[:].indirect(offsets[:]))

        def early_bank(shape, turn):
            return acc_pool.tile(shape, F32, name="early", tag=f"sum{5 + turn % 2}")

        ts_columns = tile([P, SLICES * BLOCKS], F32, "ts_columns")
        ts_spread = tile([P, S - TURNED], F32, "ts_spread")
        for s in range(SLICES):
            turned = early_bank([P, BLOCKS, P], s)
            for i in range(BLOCKS):
                c0 = s * N + i * P
                nc.tensor.transpose(turned[:, i, :], ts_picked[:, c0 : c0 + P], identity[:])
            nc.scalar.copy(ts_columns[:, s * BLOCKS : (s + 1) * BLOCKS], turned[:, :, LIVE_ROW])

        bias = tile([P, 1], F32, "bias")
        turned = early_bank([P, BLOCKS, P], SLICES)
        nc.tensor.transpose(turned[:, 0, :], bias_row[:], identity[:])
        nc.scalar.copy(bias[:], turned[:, 0, LIVE_ROW:P])

        for turn, c0 in enumerate(range(TURNED, S, N)):
            width = min(N, S - c0)
            spread = early_bank([P, width], turn)
            for i in range(width // P):
                column = c0 // P + i
                nc.tensor.transpose(
                    spread[:, i * P : (i + 1) * P],
                    ts_columns[:, column : column + 1].to_broadcast([P, P]),
                    identity[:],
                )
            nc.scalar.copy(ts_spread[:, c0 - TURNED : c0 - TURNED + width], spread[:])

        picked = [tile([P, S], U32, "picked0"), tile([P, S], U32, "picked1")]
        nc.vector.tensor_copy(picked[0][:], window0[:].bitcast(U32).indirect(offsets[:]))
        nc.vector.tensor_copy(picked[1][:], window1[:].bitcast(U32).indirect(offsets[:]))

        w_codes = tile([P, PASSES * M], U32, "w_codes")
        w_scales = tile([P, PASSES * M], U8, "w_scales")
        starts = [0, P, P + HALF, TURNED, 2 * N, S - HALF, S - P]
        widths = [c1 - c0 for c0, c1 in zip(starts, starts[1:] + [S])]
        sums = [acc_pool.tile([P, n], F32, name=f"sum{g}", tag=f"sum{g}") for g, n in enumerate(widths)]

        def quantize_w(a0, a1, rounded):
            nc.vector.quantize_mx(
                out=w_codes[:, a0 * M : a1 * M].bitcast(FP8X4), scales=w_scales[:, a0 * M : a1 * M], in_=rounded
            )

        def multiply(a, g, words, words_from, plane, plane_from):
            c0 = starts[g]
            codes, scales = w_codes[:, a * M : (a + 1) * M].bitcast(FP8X4), w_scales[:, a * M : (a + 1) * M]

            def table(t0, t1):
                return (
                    words[:, t0 - words_from : t1 - words_from].bitcast(FP8X4),
                    plane[4 * a : P, (t0 - plane_from) // 4 : (t1 - plane_from) // 4].bitcast(U8),
                )

            if c0 < TURNED:
                for i in range(widths[g] // P):
                    t_codes, t_scales = table(c0 + i * P, c0 + (i + 1) * P)
                    nc.tensor.matmul_mx(
                        out=sums[g][:, i * P : (i + 1) * P],
                        lhsT=t_codes,
                        lhsT_scale=t_scales,
                        rhs=codes,
                        rhs_scale=scales,
                        start=(a == 0 and i == 0),
                        stop=(a == PASSES - 1 and i == widths[g] // P - 1),
                    )
            else:
                odd = widths[g] % HALF if widths[g] > HALF else 0
                for p0, p1 in ((0, odd), (odd, widths[g])):
                    if p1 > p0:
                        t_codes, t_scales = table(c0 + p0, c0 + p1)
                        nc.tensor.matmul_mx(
                            out=sums[g][:, p0:p1],
                            lhsT=codes,
                            lhsT_scale=scales,
                            rhs=t_codes,
                            rhs_scale=t_scales,
                            start=(a == 0 and p0 == 0),
                            stop=(a == PASSES - 1 and p1 == widths[g]),
                        )

        def gather_pass2(c0, words):
            c1 = c0 + words.shape[1]
            nc.vector.tensor_copy(words, window2[:].bitcast(U32).indirect(offsets[:, c0 // 16 : c1 // 16]))
            return words

        quantize_w(0, 2, w_bf16_early[:].rearrange("p a c -> p (a c)"))
        for a in range(2):
            for g in range(len(starts)):
                multiply(a, g, picked[a], 0, planes[a], 0)

        scaled1_at = w_last_end + 4 * N
        scaled = [tile([P, n], F32, f"scaled{g}") for g, n in enumerate(widths[:5])]
        scaled[2] = late_tile([P, widths[2]], F32, "scaled_held", scaled1_at)
        scaled_last = tile([P, HALF], F32, "scaled_last")
        scaled[5:] = [scaled_last[:, 0:P], scaled_last[:, P:HALF]]
        result = [tile([P, n], F32, f"result{g}") for g, n in enumerate(widths[:5] + [HALF])]
        result[3] = late_tile([P, widths[3]], F32, "result_above", scaled1_at + 4 * widths[2] - 64)

        def scale_turned(g):
            for i in range(widths[g] // P):
                c0 = starts[g] + i * P
                nc.scalar.activation(
                    scaled[g][:, i * P : (i + 1) * P],
                    sums[g][:, i * P : (i + 1) * P],
                    IDENTITY,
                    scale=ts_columns[:, c0 // P : c0 // P + 1],
                )

        def turn_back(g):
            c0 = starts[g]
            back = acc_pool.tile([P, widths[g]], F32, name="back", tag=("back", "sum0", "sum1")[g])
            for i in range(widths[g] // P):
                nc.tensor.transpose(back[:, i * P : (i + 1) * P], scaled[g][:, i * P : (i + 1) * P], identity[:])
            nc.scalar.activation(result[g][:], back[:], IDENTITY, bias=bias[:])
            nc.sync.dma_start(out[:, c0 : c0 + widths[g]], result[g][:])

        first = gather_pass2(0, tile([P, TURNED], U32, "picked_first")[:])
        quantize_w(2, 3, w_bf16_last[:])
        for g in (0, 1, 2):
            multiply(2, g, first, 0, planes[2], 0)
        second = gather_pass2(TURNED, late_tile([P, widths[3]], U32, "picked_second", w_last_at + 64 - 4 * widths[3])[:])
        multiply(2, 3, second, TURNED, planes[2], 0)
        for g in (0, 1, 2):
            scale_turned(g)
        for g in (0, 1, 2):
            turn_back(g)
        third = late_tile([P, N], U32, "picked_third", w_last_end - 64)
        for h in range(2):
            gather_pass2(2 * N + h * HALF, third[:, h * HALF : (h + 1) * HALF])
        for g in (4, 5, 6):
            multiply(2, g, third, 2 * N, plane_last, 2 * N)

        def scale(g, c0=0, c1=None):
            c1 = c1 or widths[g]
            at = starts[g] - TURNED
            nc.vector.tensor_tensor(scaled[g][:, c0:c1], sums[g][:, c0:c1], ts_spread[:, at + c0 : at + c1], MULT)

        for c0, c1 in ((0, P), (P, widths[3])):
            scale(3, c0, c1)
            nc.scalar.activation(result[3][:, c0:c1], scaled[3][:, c0:c1], IDENTITY, bias=bias[:])
            nc.sync.dma_start(out[:, starts[3] + c0 : starts[3] + c1], result[3][:, c0:c1])
        for g in (4, 5, 6):
            scale(g)
        nc.vector.tensor_scalar_add(result[4][:], scaled[4][:], bias[:])
        nc.sync.dma_start(out[:, starts[4] : starts[5]], result[4][:])
        for g in (5, 6):
            c0 = starts[g] - starts[5]
            nc.vector.tensor_scalar_add(result[5][:, c0 : c0 + P], scaled[g], bias[:])
        nc.sync.dma_start(out[:, starts[5] : S], result[5][:])
